import numpy as np
import ml_dtypes


def mxq(x, axis, fmt="e4m3"):
    dtype, down = {"e4m3": (ml_dtypes.float8_e4m3fn, 7), "e5m2": (ml_dtypes.float8_e5m2, 14)}[fmt]
    v = np.moveaxis(np.asarray(x, np.float32).astype(ml_dtypes.bfloat16).astype(np.float64), axis, -1)
    blocks = v.reshape(v.shape[:-1] + (-1, 32))
    amax = np.abs(blocks).max(-1, keepdims=True)
    byte = np.maximum(np.where(amax > 0, np.frexp(amax)[1] - 1 + 127, 0) - down, 1)
    scale = np.exp2(byte - 127.0)
    codes = (blocks / scale).astype(np.float32).astype(dtype).astype(np.float64)
    return np.moveaxis((codes * scale).reshape(v.shape), -1, axis)


WIDE = False


def mx_kscale(k):
    if not WIDE:
        return np.ones(k)
    levels = np.array([10, -10, 5, -5, 0])
    if k % 512:
        return np.exp2(np.random.permutation(np.resize(levels, k // 32))).repeat(32)
    a = np.empty((k // 512, 16))
    for p in range(k // 512):
        a[p, :8] = np.random.permutation(np.resize(levels, 8))
        for g in range(8):
            far = levels[np.abs(levels - a[p, g]) >= 10]
            a[p, g + 8] = far[np.random.randint(len(far))]
    return np.exp2(a.ravel()).repeat(32)


def f64(x):
    return np.asarray(x).astype(np.float64)


def striped(idx):
    return np.tile(idx.reshape(-1, 16).T, (8, 1)).astype(np.uint16)


def unstriped(offs):
    return offs[:16].T.reshape(-1).astype(np.int64)


E2M1 = np.array([0.0, 0.5, 1.0, 1.5, 2.0, 3.0, 4.0, 6.0, -0.0, -0.5, -1.0, -1.5, -2.0, -3.0, -4.0, -6.0])


def pack_weight(w, fmt):
    k, n = w.shape
    w = f64(np.asarray(w, np.float32).astype(ml_dtypes.bfloat16)).reshape(k // 32, 32, n)
    amax = np.abs(w).max(1)
    if fmt == "e4m3":
        byte = np.frexp(amax)[1] - 1 + 127 - 7
    else:
        mant, ex = np.frexp(amax / 6.0)
        byte = np.where(mant > 0.5, ex, ex - 1) + 127
    byte = np.clip(np.where(amax > 0, byte, 1), 1, 254)
    scaled = (w * np.exp2(127.0 - byte)[:, None, :]).reshape(k, n).astype(np.float32)
    by_word = np.ascontiguousarray(scaled.reshape(k // 512, 128, 4, n).transpose(0, 1, 3, 2))
    if fmt == "e4m3":
        words = by_word.astype(ml_dtypes.float8_e4m3fn).view(np.uint8)
    else:
        c = by_word.astype(ml_dtypes.float4_e2m1fn).view(np.uint8) & 0xF
        words = (c[..., 0::2] | (c[..., 1::2] << 4)).reshape(k // 512, 128, 2 * n)
    return np.ascontiguousarray(words), np.ascontiguousarray(byte.astype(np.uint8).reshape(k // 512, 16, n))


def unpack_weight(words, scales, fmt):
    g, _, n = scales.shape
    words = np.ascontiguousarray(words).reshape(g, 128, n, -1)
    if fmt == "e4m3":
        vals = words.view(ml_dtypes.float8_e4m3fn).astype(np.float64)
    else:
        nib = np.empty((g, 128, n, 4), np.uint8)
        nib[..., 0::2] = words & 0xF
        nib[..., 1::2] = words >> 4
        vals = E2M1[nib]
    vals = vals * np.repeat(np.exp2(scales.astype(np.float64) - 127.0), 8, axis=1)[..., None]
    return vals.transpose(0, 1, 3, 2).reshape(g * 512, n)


def pack_table(v):
    words, scales = pack_weight(v, "e4m3")
    return np.concatenate([words.reshape(words.shape[0], -1), scales.reshape(scales.shape[0], -1)], axis=1)


def unpack_table(tab):
    g, t = tab.shape[0], tab.shape[1] // 528
    return unpack_weight(tab[:, :512 * t].reshape(g, 128, t, 4), tab[:, 512 * t:].reshape(g, 16, t), "e4m3")


K, M, T, S = 1536, 128, 4096, 1536


def setup_inputs():
    n = np.random.standard_normal
    s = mx_kscale(K)[:, None]
    return {
        "tab": pack_table(n((K, T)) * s),
        "w": (n((K, M)) / np.sqrt(K) / s).astype(np.float32),
        "b": (0.3 * n(128)).astype(np.float32),
        "offs": striped(np.random.permutation(T)[:S]),
    }


def reference(tab, w, b, offs):
    tab_ = unpack_table(tab)[:, unstriped(offs)]
    w_ = mxq(f64(w), 0, "e4m3")
    y = w_.T @ tab_
    return y + f64(b)[:, None]

@@ -1,0 +1,133 @@
+import concourse.mybir as mybir
+
+K, M, T, S = 1536, 128, 4096, 1536
+FLOPS = 2 * K * M * S
+
+F32 = mybir.dt.float32
+BF16 = mybir.dt.bfloat16
+I32 = mybir.dt.int32
+U32 = mybir.dt.uint32
+U16 = mybir.dt.uint16
+U8 = mybir.dt.uint8
+FP8X4 = mybir.dt.float8_e4m3fn_x4
+IDENTITY = mybir.ActivationFunctionType.Identity
+ADD = mybir.AluOpType.add
+
+P = 128
+PASSES = K // 512
+
+
+def tile_list_tabw_bias_kernel(tc, tab, w, b, offs, out):
+    nc = tc.nc
+    with (
+        tc.tile_pool(name="lists", bufs=1) as lists,
+        tc.tile_pool(name="keep", bufs=1) as keep,
+        tc.psum_pool(name="psum", bufs=1) as psum,
+    ):
+        offsets = lists.tile([P, S // 16], U16, name="offsets")
+        words = [keep.tile([P, T], I32, name=f"words{a}", align_bytes=64) for a in range(PASSES)]
+        scales = keep.tile([P, T // 4], I32, name="scales", tag="shared", align_bytes=64)
+        picked_scales = keep.tile([P, S], U8, name="picked_scales", align_bytes=64)
+        w_raw = [keep.tile([P, 4, M], F32, name=f"w_raw{a}", align_bytes=64) for a in range(PASSES)]
+        w_bf = keep.tile([P, PASSES, M, 4], BF16, name="w_bf", align_bytes=64)
+        w_codes = keep.tile([P, PASSES * M], U32, name="w_codes", align_bytes=64)
+        w_scales = keep.tile([P, PASSES * M], U8, name="w_scales", align_bytes=64)
+        b_raw = keep.tile([P, 1], F32, name="b_raw")
+        bias = keep.tile([P, 1], F32, name="bias")
+
+        def load_words(a):
+            nc.sync.dma_start(
+                words[a][:],
+                tab[a, 0 : 512 * T].bitcast(I32).rearrange("(p t) -> p t", p=P),
+            )
+
+        def load_w(a):
+            nc.sync.dma_start(
+                w_raw[a][:], w[512 * a : 512 * (a + 1), :].rearrange("(p j) n -> p j n", j=4)
+            )
+
+        scale_rows = tab[:, 512 * T : 528 * T].bitcast(I32).rearrange("a (q t) -> a q t", q=16)
+
+        nc.vector.memset(scales[:], 0)
+        for a in range(PASSES):
+            nc.vector.memset(words[a][:, 0:8], 0)
+        nc.sync.dma_start(offsets[:], offs)
+        for a in range(PASSES):
+            load_w(a)
+        for quad in range(4):
+            queue = nc.sync if quad % 2 == 0 else nc.scalar
+            queue.dma_start(
+                scales[32 * quad : 32 * quad + 12, :], scale_rows[:, 4 * quad : 4 * quad + 4, :]
+            )
+        load_words(0)
+        nc.scalar.dma_start(b_raw[:], b.rearrange("(n one) -> n one", one=1))
+        nc.scalar.activation(bias[:], b_raw[:], IDENTITY)
+        load_words(1)
+        load_words(2)
+
+        picked = []
+
+        def pick_words(a, j0, j1):
+            nc.vector.tensor_copy(
+                picked[a][:, j0:j1],
+                words[a][:].bitcast(U32).indirect(offsets[:, j0 // 16 : j1 // 16]),
+            )
+
+        def round_w(a):
+            nc.vector.tensor_copy(w_bf[:, a], w_raw[a][:].rearrange("p j n -> p n j"))
+
+        def quantise_w(a0, a1):
+            nc.vector.quantize_mx(
+                out=w_codes[:, M * a0 : M * a1].bitcast(FP8X4),
+                scales=w_scales[:, M * a0 : M * a1],
+                in_=w_bf[:, a0:a1].rearrange("p a n j -> p (a n j)"),
+            )
+
+        pieces = [(0, 512), (512, 1024), (1024, 1280), (1280, 1536)]
+        accs = [psum.tile([M, j1 - j0], F32, name=f"acc{j0}") for j0, j1 in pieces]
+
+        def multiply(a, i):
+            j0, j1 = pieces[i]
+            nc.tensor.matmul_mx(
+                out=accs[i][:],
+                lhsT=w_codes[:, M * a : M * (a + 1)].bitcast(FP8X4),
+                lhsT_scale=w_scales[:, M * a : M * (a + 1)],
+                rhs=picked[a][:, j0:j1].bitcast(FP8X4),
+                rhs_scale=picked_scales[4 * a : P, j0:j1],
+                start=(a == 0),
+                stop=(a == PASSES - 1),
+            )
+
+        results = [keep.tile([M, j1 - j0], F32, name=f"result{j0}") for j0, j1 in pieces]
+
+        def finish(i, on_vector, queue):
+            j0, j1 = pieces[i]
+            if on_vector:
+                nc.vector.tensor_scalar(results[i][:], accs[i][:], bias[:], None, op0=ADD)
+            else:
+                nc.scalar.activation(results[i][:], accs[i][:], IDENTITY, bias=bias[:])
+            queue.dma_start(out[:, j0:j1], results[i][:])
+
+        for a in range(PASSES):
+            round_w(a)
+        quantise_w(0, 2)
+        quantise_w(2, 3)
+        nc.vector.tensor_copy(picked_scales[:], scales[:].bitcast(U8).indirect(offsets[:]))
+        picked.append(keep.tile([P, S], U32, name="picked0", tag="shared", align_bytes=64))
+        for a in range(1, PASSES):
+            picked.append(keep.tile([P, S], U32, name=f"picked{a}", align_bytes=64))
+        for a in range(2):
+            pick_words(a, 0, S)
+            for i in range(4):
+                multiply(a, i)
+        pick_words(2, 0, 512)
+        multiply(2, 0)
+        finish(0, False, nc.sync)
+        pick_words(2, 512, 1024)
+        multiply(2, 1)
+        finish(1, False, nc.sync)
+        pick_words(2, 1024, S)
+        multiply(2, 2)
+        multiply(2, 3)
+        finish(2, False, nc.scalar)
+        finish(3, True, nc.sync)

@@ -17,6 +17,9 @@ P = 128
 PASSES = K // 512
 
 
+ROW_BASE = (0, 16, 64)
+
+
 def tile_list_tabw_bias_kernel(tc, tab, w, b, offs, out):
     nc = tc.nc
     with (
@@ -26,8 +29,10 @@ def tile_list_tabw_bias_kernel(tc, tab, w, b, offs, out):
     ):
         offsets = lists.tile([P, S // 16], U16, name="offsets")
         words = [keep.tile([P, T], I32, name=f"words{a}", align_bytes=64) for a in range(PASSES)]
-        scales = keep.tile([P, T // 4], I32, name="scales", tag="shared", align_bytes=64)
-        picked_scales = keep.tile([P, S], U8, name="picked_scales", align_bytes=64)
+        scales = keep.tile([P, T // 4], I32, name="scales", align_bytes=64)
+        picked_rows = keep.tile([P, S // 4], I32, name="picked_rows", align_bytes=64)
+        planes = keep.tile([P, PASSES * S // 4], I32, name="planes", align_bytes=64)
+        picked = [keep.tile([P, S], U32, name=f"picked{a}", align_bytes=64) for a in range(PASSES)]
         w_raw = [keep.tile([P, 4, M], F32, name=f"w_raw{a}", align_bytes=64) for a in range(PASSES)]
         w_bf = keep.tile([P, PASSES, M, 4], BF16, name="w_bf", align_bytes=64)
         w_codes = keep.tile([P, PASSES * M], U32, name="w_codes", align_bytes=64)
@@ -35,37 +40,33 @@ def tile_list_tabw_bias_kernel(tc, tab, w, b, offs, out):
         b_raw = keep.tile([P, 1], F32, name="b_raw")
         bias = keep.tile([P, 1], F32, name="bias")
 
-        def load_words(a):
-            nc.sync.dma_start(
-                words[a][:],
-                tab[a, 0 : 512 * T].bitcast(I32).rearrange("(p t) -> p t", p=P),
-            )
+        scale_rows = tab[:, 512 * T : 528 * T].bitcast(I32).rearrange("a (q t) -> a q t", q=16)
+
+        def load_scales(a):
+            nc.sync.dma_start(scales[ROW_BASE[a] : ROW_BASE[a] + 16, :], scale_rows[a])
 
         def load_w(a):
             nc.sync.dma_start(
                 w_raw[a][:], w[512 * a : 512 * (a + 1), :].rearrange("(p j) n -> p j n", j=4)
             )
 
-        scale_rows = tab[:, 512 * T : 528 * T].bitcast(I32).rearrange("a (q t) -> a q t", q=16)
-
-        nc.vector.memset(scales[:], 0)
-        for a in range(PASSES):
-            nc.vector.memset(words[a][:, 0:8], 0)
+        nc.vector.memset(scales[64:P, :], 0)
+        nc.vector.memset(scales[32:64, :], 0)
+        nc.vector.memset(planes[:], 0)
         nc.sync.dma_start(offsets[:], offs)
+        load_scales(0)
+        load_scales(1)
+        load_w(0)
+        load_scales(2)
+        load_w(1)
+        load_w(2)
         for a in range(PASSES):
-            load_w(a)
-        for quad in range(4):
-            queue = nc.sync if quad % 2 == 0 else nc.scalar
-            queue.dma_start(
-                scales[32 * quad : 32 * quad + 12, :], scale_rows[:, 4 * quad : 4 * quad + 4, :]
+            nc.sync.dma_start(
+                words[a][:],
+                tab[a, 0 : 512 * T].bitcast(I32).rearrange("(p t) -> p t", p=P),
             )
-        load_words(0)
-        nc.scalar.dma_start(b_raw[:], b.rearrange("(n one) -> n one", one=1))
+        nc.gpsimd.dma_start(b_raw[:], b.rearrange("(n one) -> n one", one=1))
         nc.scalar.activation(bias[:], b_raw[:], IDENTITY)
-        load_words(1)
-        load_words(2)
-
-        picked = []
 
         def pick_words(a, j0, j1):
             nc.vector.tensor_copy(
@@ -73,15 +74,21 @@ def tile_list_tabw_bias_kernel(tc, tab, w, b, offs, out):
                 words[a][:].bitcast(U32).indirect(offsets[:, j0 // 16 : j1 // 16]),
             )
 
-        def round_w(a):
-            nc.vector.tensor_copy(w_bf[:, a], w_raw[a][:].rearrange("p j n -> p n j"))
-
         def quantise_w(a0, a1):
             nc.vector.quantize_mx(
                 out=w_codes[:, M * a0 : M * a1].bitcast(FP8X4),
                 scales=w_scales[:, M * a0 : M * a1],
                 in_=w_bf[:, a0:a1].rearrange("p a n j -> p (a n j)"),
             )
+
+        def place_scales(a, queue):
+            for quad in range(4):
+                src = ROW_BASE[a] + 4 * quad
+                dst = 32 * quad + 4 * a
+                queue.dma_start(
+                    planes[dst : dst + 4, a * S // 4 : (a + 1) * S // 4],
+                    picked_rows[src : src + 4, :],
+                )
 
         pieces = [(0, 512), (512, 1024), (1024, 1280), (1280, 1536)]
         accs = [psum.tile([M, j1 - j0], F32, name=f"acc{j0}") for j0, j1 in pieces]
@@ -93,7 +100,7 @@ def tile_list_tabw_bias_kernel(tc, tab, w, b, offs, out):
                 lhsT=w_codes[:, M * a : M * (a + 1)].bitcast(FP8X4),
                 lhsT_scale=w_scales[:, M * a : M * (a + 1)],
                 rhs=picked[a][:, j0:j1].bitcast(FP8X4),
-                rhs_scale=picked_scales[4 * a : P, j0:j1],
+                rhs_scale=planes[:].bitcast(U8)[4 * a : P, a * S + j0 : a * S + j1],
                 start=(a == 0),
                 stop=(a == PASSES - 1),
             )
@@ -108,14 +115,16 @@ def tile_list_tabw_bias_kernel(tc, tab, w, b, offs, out):
                 nc.scalar.activation(results[i][:], accs[i][:], IDENTITY, bias=bias[:])
             queue.dma_start(out[:, j0:j1], results[i][:])
 
+        nc.vector.tensor_copy(
+            picked_rows[:].bitcast(U8), scales[:].bitcast(U8).indirect(offsets[:])
+        )
         for a in range(PASSES):
-            round_w(a)
+            nc.scalar.copy(w_bf[:, a], w_raw[a][:].rearrange("p j n -> p n j"))
         quantise_w(0, 2)
         quantise_w(2, 3)
-        nc.vector.tensor_copy(picked_scales[:], scales[:].bitcast(U8).indirect(offsets[:]))
-        picked.append(keep.tile([P, S], U32, name="picked0", tag="shared", align_bytes=64))
-        for a in range(1, PASSES):
-            picked.append(keep.tile([P, S], U32, name=f"picked{a}", align_bytes=64))
+        place_scales(0, nc.scalar)
+        place_scales(1, nc.gpsimd)
+        place_scales(2, nc.scalar)
         for a in range(2):
             pick_words(a, 0, S)
             for i in range(4):

@@ -25,11 +25,15 @@ def tile_list_tabw_bias_kernel(tc, tab, w, b, offs, out):
     with (
         tc.tile_pool(name="lists", bufs=1) as lists,
         tc.tile_pool(name="keep", bufs=1) as keep,
+        tc.tile_pool(name="late", bufs=1) as late,
         tc.psum_pool(name="psum", bufs=1) as psum,
     ):
         offsets = lists.tile([P, S // 16], U16, name="offsets")
-        words = [keep.tile([P, T], I32, name=f"words{a}", align_bytes=64) for a in range(PASSES)]
-        scales = keep.tile([P, T // 4], I32, name="scales", align_bytes=64)
+        scales = late.tile([P, T // 4], I32, name="scales", align_bytes=64, offset=4 * T - T // 2)
+        words = [keep.tile([P, T], I32, name="words0", align_bytes=64)] + [
+            late.tile([P, T], I32, name=f"words{a}", align_bytes=64, offset=4 * T * (a - 1))
+            for a in range(1, PASSES)
+        ]
         picked_rows = keep.tile([P, S // 4], I32, name="picked_rows", align_bytes=64)
         planes = keep.tile([P, PASSES * S // 4], I32, name="planes", align_bytes=64)
         picked = [keep.tile([P, S], U32, name=f"picked{a}", align_bytes=64) for a in range(PASSES)]
@@ -37,13 +41,18 @@ def tile_list_tabw_bias_kernel(tc, tab, w, b, offs, out):
         w_bf = keep.tile([P, PASSES, M, 4], BF16, name="w_bf", align_bytes=64)
         w_codes = keep.tile([P, PASSES * M], U32, name="w_codes", align_bytes=64)
         w_scales = keep.tile([P, PASSES * M], U8, name="w_scales", align_bytes=64)
-        b_raw = keep.tile([P, 1], F32, name="b_raw")
         bias = keep.tile([P, 1], F32, name="bias")
 
         scale_rows = tab[:, 512 * T : 528 * T].bitcast(I32).rearrange("a (q t) -> a q t", q=16)
 
         def load_scales(a):
             nc.sync.dma_start(scales[ROW_BASE[a] : ROW_BASE[a] + 16, :], scale_rows[a])
+
+        def load_words(a):
+            nc.sync.dma_start(
+                words[a][:],
+                tab[a, 0 : 512 * T].bitcast(I32).rearrange("(p t) -> p t", p=P),
+            )
 
         def load_w(a):
             nc.sync.dma_start(
@@ -53,20 +62,14 @@ def tile_list_tabw_bias_kernel(tc, tab, w, b, offs, out):
         nc.vector.memset(scales[64:P, :], 0)
         nc.vector.memset(scales[32:64, :], 0)
         nc.vector.memset(planes[:], 0)
-        nc.sync.dma_start(offsets[:], offs)
         load_scales(0)
         load_scales(1)
-        load_w(0)
+        nc.sync.dma_start(offsets[:], offs)
         load_scales(2)
-        load_w(1)
-        load_w(2)
         for a in range(PASSES):
-            nc.sync.dma_start(
-                words[a][:],
-                tab[a, 0 : 512 * T].bitcast(I32).rearrange("(p t) -> p t", p=P),
-            )
-        nc.gpsimd.dma_start(b_raw[:], b.rearrange("(n one) -> n one", one=1))
-        nc.scalar.activation(bias[:], b_raw[:], IDENTITY)
+            load_w(a)
+        load_words(0)
+        nc.scalar.dma_start(bias[:], b.rearrange("(n one) -> n one", one=1))
 
         def pick_words(a, j0, j1):
             nc.vector.tensor_copy(
@@ -122,9 +125,10 @@ def tile_list_tabw_bias_kernel(tc, tab, w, b, offs, out):
             nc.scalar.copy(w_bf[:, a], w_raw[a][:].rearrange("p j n -> p n j"))
         quantise_w(0, 2)
         quantise_w(2, 3)
-        place_scales(0, nc.scalar)
-        place_scales(1, nc.gpsimd)
-        place_scales(2, nc.scalar)
+        for a in range(PASSES):
+            place_scales(a, nc.sync)
+            if a + 1 < PASSES:
+                load_words(a + 1)
         for a in range(2):
             pick_words(a, 0, S)
             for i in range(4):

@@ -29,19 +29,19 @@ def tile_list_tabw_bias_kernel(tc, tab, w, b, offs, out):
         tc.psum_pool(name="psum", bufs=1) as psum,
     ):
         offsets = lists.tile([P, S // 16], U16, name="offsets")
-        scales = late.tile([P, T // 4], I32, name="scales", align_bytes=64, offset=4 * T - T // 2)
-        words = [keep.tile([P, T], I32, name="words0", align_bytes=64)] + [
-            late.tile([P, T], I32, name=f"words{a}", align_bytes=64, offset=4 * T * (a - 1))
+        scales = late.tile([P, T // 4], I32, name="scales", align_bytes=512, offset=4 * T - T // 2)
+        words = [keep.tile([P, T], I32, name="words0", align_bytes=512)] + [
+            late.tile([P, T], I32, name=f"words{a}", align_bytes=512, offset=(4 * T + 512) * (a - 1))
             for a in range(1, PASSES)
         ]
-        picked_rows = keep.tile([P, S // 4], I32, name="picked_rows", align_bytes=64)
-        planes = keep.tile([P, PASSES * S // 4], I32, name="planes", align_bytes=64)
-        picked = [keep.tile([P, S], U32, name=f"picked{a}", align_bytes=64) for a in range(PASSES)]
-        w_raw = [keep.tile([P, 4, M], F32, name=f"w_raw{a}", align_bytes=64) for a in range(PASSES)]
-        w_bf = keep.tile([P, PASSES, M, 4], BF16, name="w_bf", align_bytes=64)
-        w_codes = keep.tile([P, PASSES * M], U32, name="w_codes", align_bytes=64)
-        w_scales = keep.tile([P, PASSES * M], U8, name="w_scales", align_bytes=64)
-        bias = keep.tile([P, 1], F32, name="bias")
+        picked_rows = keep.tile([P, S // 4], I32, name="picked_rows", align_bytes=512)
+        planes = keep.tile([P, PASSES * S // 4], I32, name="planes", align_bytes=512)
+        picked = [keep.tile([P, S], U32, name=f"picked{a}", align_bytes=512) for a in range(PASSES)]
+        w_raw = [keep.tile([P, 4, M], F32, name=f"w_raw{a}", align_bytes=512) for a in range(PASSES)]
+        w_bf = keep.tile([P, PASSES, M, 4], BF16, name="w_bf", align_bytes=512)
+        w_codes = keep.tile([P, PASSES * M], U32, name="w_codes", align_bytes=512)
+        w_scales = keep.tile([P, PASSES * M], U8, name="w_scales", align_bytes=512)
+        bias = late.tile([P, 1], F32, name="bias", align_bytes=512, offset=4 * T)
 
         scale_rows = tab[:, 512 * T : 528 * T].bitcast(I32).rearrange("a (q t) -> a q t", q=16)
 
@@ -69,7 +69,6 @@ def tile_list_tabw_bias_kernel(tc, tab, w, b, offs, out):
         for a in range(PASSES):
             load_w(a)
         load_words(0)
-        nc.scalar.dma_start(bias[:], b.rearrange("(n one) -> n one", one=1))
 
         def pick_words(a, j0, j1):
             nc.vector.tensor_copy(
@@ -108,7 +107,7 @@ def tile_list_tabw_bias_kernel(tc, tab, w, b, offs, out):
                 stop=(a == PASSES - 1),
             )
 
-        results = [keep.tile([M, j1 - j0], F32, name=f"result{j0}") for j0, j1 in pieces]
+        results = [keep.tile([M, j1 - j0], F32, name=f"result{j0}", align_bytes=512) for j0, j1 in pieces]
 
         def finish(i, on_vector, queue):
             j0, j1 = pieces[i]
@@ -125,13 +124,14 @@ def tile_list_tabw_bias_kernel(tc, tab, w, b, offs, out):
             nc.scalar.copy(w_bf[:, a], w_raw[a][:].rearrange("p j n -> p n j"))
         quantise_w(0, 2)
         quantise_w(2, 3)
-        for a in range(PASSES):
+        for a in range(PASSES - 1):
             place_scales(a, nc.sync)
-            if a + 1 < PASSES:
-                load_words(a + 1)
+            load_words(a + 1)
+        place_scales(PASSES - 1, nc.sync)
+        nc.sync.dma_start(bias[:], b.rearrange("(n one) -> n one", one=1))
         for a in range(2):
             pick_words(a, 0, S)
-            for i in range(4):
+            for i in range(len(pieces)):
                 multiply(a, i)
         pick_words(2, 0, 512)
         multiply(2, 0)

@@ -18,6 +18,7 @@ PASSES = K // 512
 
 
 ROW_BASE = (0, 16, 64)
+THIRD = S // 3
 
 
 def tile_list_tabw_bias_kernel(tc, tab, w, b, offs, out):
@@ -26,22 +27,31 @@ def tile_list_tabw_bias_kernel(tc, tab, w, b, offs, out):
         tc.tile_pool(name="lists", bufs=1) as lists,
         tc.tile_pool(name="keep", bufs=1) as keep,
         tc.tile_pool(name="late", bufs=1) as late,
+        tc.tile_pool(name="last", bufs=1) as last,
         tc.psum_pool(name="psum", bufs=1) as psum,
     ):
         offsets = lists.tile([P, S // 16], U16, name="offsets")
-        scales = late.tile([P, T // 4], I32, name="scales", align_bytes=512, offset=4 * T - T // 2)
-        words = [keep.tile([P, T], I32, name="words0", align_bytes=512)] + [
-            late.tile([P, T], I32, name=f"words{a}", align_bytes=512, offset=(4 * T + 512) * (a - 1))
-            for a in range(1, PASSES)
+        scales = late.tile([P, T // 4], I32, name="scales", align_bytes=64, offset=0)
+        w_raw = [late.tile([P, 4, M], F32, name="w_raw0", align_bytes=64, offset=0)] + [
+            keep.tile([P, 4, M], F32, name=f"w_raw{a}", align_bytes=64) for a in (1, 2)
         ]
-        picked_rows = keep.tile([P, S // 4], I32, name="picked_rows", align_bytes=512)
-        planes = keep.tile([P, PASSES * S // 4], I32, name="planes", align_bytes=512)
-        picked = [keep.tile([P, S], U32, name=f"picked{a}", align_bytes=512) for a in range(PASSES)]
-        w_raw = [keep.tile([P, 4, M], F32, name=f"w_raw{a}", align_bytes=512) for a in range(PASSES)]
-        w_bf = keep.tile([P, PASSES, M, 4], BF16, name="w_bf", align_bytes=512)
-        w_codes = keep.tile([P, PASSES * M], U32, name="w_codes", align_bytes=512)
-        w_scales = keep.tile([P, PASSES * M], U8, name="w_scales", align_bytes=512)
-        bias = late.tile([P, 1], F32, name="bias", align_bytes=512, offset=4 * T)
+        bias = late.tile([P, 1], F32, name="bias", align_bytes=64, offset=16 * M)
+        words = [keep.tile([P, T], I32, name=f"words{a}", align_bytes=64) for a in (0, 1)] + [
+            late.tile([P, T], I32, name="words2", align_bytes=64, offset=16 * M + 64)
+        ]
+        picked_rows = keep.tile([P, S // 4], I32, name="picked_rows", align_bytes=64)
+        planes = keep.tile([P, PASSES * S // 4], I32, name="planes", align_bytes=64)
+        picked = [keep.tile([P, S], U32, name=f"picked{a}", align_bytes=64) for a in (0, 1)]
+        w_bf_early = keep.tile([P, 2, M, 4], BF16, name="w_bf_early", align_bytes=64)
+        w_bf_late = last.tile(
+            [P, M, 4], BF16, name="w_bf_late", align_bytes=64, offset=8 * THIRD - 4 * M
+        )
+        picked_last = [
+            last.tile([P, THIRD], U32, name=f"picked_last{i}", align_bytes=64, offset=4 * THIRD * i)
+            for i in range(3)
+        ]
+        w_codes = keep.tile([P, PASSES * M], U32, name="w_codes", align_bytes=64)
+        w_scales = keep.tile([P, PASSES * M], U8, name="w_scales", align_bytes=64)
 
         scale_rows = tab[:, 512 * T : 528 * T].bitcast(I32).rearrange("a (q t) -> a q t", q=16)
 
@@ -59,55 +69,50 @@ def tile_list_tabw_bias_kernel(tc, tab, w, b, offs, out):
                 w_raw[a][:], w[512 * a : 512 * (a + 1), :].rearrange("(p j) n -> p j n", j=4)
             )
 
-        nc.vector.memset(scales[64:P, :], 0)
-        nc.vector.memset(scales[32:64, :], 0)
-        nc.vector.memset(planes[:], 0)
-        load_scales(0)
-        load_scales(1)
-        nc.sync.dma_start(offsets[:], offs)
-        load_scales(2)
-        for a in range(PASSES):
-            load_w(a)
-        load_words(0)
-
-        def pick_words(a, j0, j1):
+        def pick_words(dst, a, j0, j1):
             nc.vector.tensor_copy(
-                picked[a][:, j0:j1],
-                words[a][:].bitcast(U32).indirect(offsets[:, j0 // 16 : j1 // 16]),
+                dst, words[a][:].bitcast(U32).indirect(offsets[:, j0 // 16 : j1 // 16])
             )
 
-        def quantise_w(a0, a1):
+        def round_w(dst, a):
+            nc.scalar.copy(dst, w_raw[a][:].rearrange("p j n -> p n j"))
+
+        def quantise_w(src, a0, a1):
             nc.vector.quantize_mx(
                 out=w_codes[:, M * a0 : M * a1].bitcast(FP8X4),
                 scales=w_scales[:, M * a0 : M * a1],
-                in_=w_bf[:, a0:a1].rearrange("p a n j -> p (a n j)"),
+                in_=src,
             )
 
-        def place_scales(a, queue):
+        def place_scales(a):
             for quad in range(4):
                 src = ROW_BASE[a] + 4 * quad
                 dst = 32 * quad + 4 * a
-                queue.dma_start(
+                nc.sync.dma_start(
                     planes[dst : dst + 4, a * S // 4 : (a + 1) * S // 4],
                     picked_rows[src : src + 4, :],
                 )
 
         pieces = [(0, 512), (512, 1024), (1024, 1280), (1280, 1536)]
         accs = [psum.tile([M, j1 - j0], F32, name=f"acc{j0}") for j0, j1 in pieces]
+        results = [keep.tile([M, j1 - j0], F32, name=f"result{j0}") for j0, j1 in pieces]
 
         def multiply(a, i):
             j0, j1 = pieces[i]
+            if a < 2:
+                codes = picked[a][:, j0:j1]
+            else:
+                third = j0 // THIRD
+                codes = picked_last[third][:, j0 - third * THIRD : j1 - third * THIRD]
             nc.tensor.matmul_mx(
                 out=accs[i][:],
                 lhsT=w_codes[:, M * a : M * (a + 1)].bitcast(FP8X4),
                 lhsT_scale=w_scales[:, M * a : M * (a + 1)],
-                rhs=picked[a][:, j0:j1].bitcast(FP8X4),
+                rhs=codes.bitcast(FP8X4),
                 rhs_scale=planes[:].bitcast(U8)[4 * a : P, a * S + j0 : a * S + j1],
-                start=(a == 0),
-                stop=(a == PASSES - 1),
+                start=(a == 1),
+                stop=(a == 2),
             )
-
-        results = [keep.tile([M, j1 - j0], F32, name=f"result{j0}", align_bytes=512) for j0, j1 in pieces]
 
         def finish(i, on_vector, queue):
             j0, j1 = pieces[i]
@@ -117,29 +122,48 @@ def tile_list_tabw_bias_kernel(tc, tab, w, b, offs, out):
                 nc.scalar.activation(results[i][:], accs[i][:], IDENTITY, bias=bias[:])
             queue.dma_start(out[:, j0:j1], results[i][:])
 
+        nc.vector.memset(scales[64:P, :], 0)
+        nc.vector.memset(scales[32:64, :], 0)
+        nc.vector.memset(planes[:], 0)
+        load_scales(0)
+        load_scales(1)
+        nc.sync.dma_start(offsets[:], offs)
+        load_scales(2)
+        load_w(1)
+        load_w(2)
+        load_words(0)
+        load_words(1)
+
         nc.vector.tensor_copy(
             picked_rows[:].bitcast(U8), scales[:].bitcast(U8).indirect(offsets[:])
         )
-        for a in range(PASSES):
-            nc.scalar.copy(w_bf[:, a], w_raw[a][:].rearrange("p j n -> p n j"))
-        quantise_w(0, 2)
-        quantise_w(2, 3)
-        for a in range(PASSES - 1):
-            place_scales(a, nc.sync)
-            load_words(a + 1)
-        place_scales(PASSES - 1, nc.sync)
+        for a in (1, 2):
+            round_w(w_bf_early[:, a - 1], a)
+        quantise_w(w_bf_early[:].rearrange("p a n j -> p (a n j)"), 1, 3)
+        place_scales(1)
+        load_words(2)
+        load_w(0)
+        place_scales(0)
+        place_scales(2)
         nc.sync.dma_start(bias[:], b.rearrange("(n one) -> n one", one=1))
-        for a in range(2):
-            pick_words(a, 0, S)
-            for i in range(len(pieces)):
-                multiply(a, i)
-        pick_words(2, 0, 512)
+
+        for a in (0, 1):
+            pick_words(picked[a][:], a, 0, S)
+        for i in range(len(pieces)):
+            multiply(1, i)
+        pick_words(picked_last[0][:], 2, 0, THIRD)
+        round_w(w_bf_late[:], 0)
+        quantise_w(w_bf_late[:].rearrange("p n j -> p (n j)"), 0, 1)
+        multiply(0, 0)
         multiply(2, 0)
         finish(0, False, nc.sync)
-        pick_words(2, 512, 1024)
+        pick_words(picked_last[1][:], 2, THIRD, 2 * THIRD)
+        multiply(0, 1)
         multiply(2, 1)
         finish(1, False, nc.sync)
-        pick_words(2, 1024, S)
+        multiply(0, 2)
+        multiply(0, 3)
+        pick_words(picked_last[2][:], 2, 2 * THIRD, S)
         multiply(2, 2)
         multiply(2, 3)
         finish(2, False, nc.scalar)

@@ -17,7 +17,8 @@ P = 128
 PASSES = K // 512
 
 
-ROW_BASE = (0, 16, 64)
+ROW_BASE = (32, 33, 34)
+ROW_STEP = 4
 THIRD = S // 3
 
 
@@ -35,9 +36,9 @@ def tile_list_tabw_bias_kernel(tc, tab, w, b, offs, out):
         w_raw = [late.tile([P, 4, M], F32, name="w_raw0", align_bytes=64, offset=0)] + [
             keep.tile([P, 4, M], F32, name=f"w_raw{a}", align_bytes=64) for a in (1, 2)
         ]
-        bias = late.tile([P, 1], F32, name="bias", align_bytes=64, offset=16 * M)
+        bias = keep.tile([P, 1], F32, name="bias")
         words = [keep.tile([P, T], I32, name=f"words{a}", align_bytes=64) for a in (0, 1)] + [
-            late.tile([P, T], I32, name="words2", align_bytes=64, offset=16 * M + 64)
+            late.tile([P, T], I32, name="words2", align_bytes=64, offset=16 * M)
         ]
         picked_rows = keep.tile([P, S // 4], I32, name="picked_rows", align_bytes=64)
         planes = keep.tile([P, PASSES * S // 4], I32, name="planes", align_bytes=64)
@@ -56,7 +57,7 @@ def tile_list_tabw_bias_kernel(tc, tab, w, b, offs, out):
         scale_rows = tab[:, 512 * T : 528 * T].bitcast(I32).rearrange("a (q t) -> a q t", q=16)
 
         def load_scales(a):
-            nc.sync.dma_start(scales[ROW_BASE[a] : ROW_BASE[a] + 16, :], scale_rows[a])
+            nc.sync.dma_start(scales[ROW_BASE[a] : ROW_BASE[a] + 16 * ROW_STEP : ROW_STEP, :], scale_rows[a])
 
         def load_words(a):
             nc.sync.dma_start(
@@ -86,11 +87,11 @@ def tile_list_tabw_bias_kernel(tc, tab, w, b, offs, out):
 
         def place_scales(a):
             for quad in range(4):
-                src = ROW_BASE[a] + 4 * quad
+                src = ROW_BASE[a] + 4 * ROW_STEP * quad
                 dst = 32 * quad + 4 * a
                 nc.sync.dma_start(
                     planes[dst : dst + 4, a * S // 4 : (a + 1) * S // 4],
-                    picked_rows[src : src + 4, :],
+                    picked_rows[src : src + 4 * ROW_STEP : ROW_STEP, :],
                 )
 
         pieces = [(0, 512), (512, 1024), (1024, 1280), (1280, 1536)]
@@ -122,14 +123,13 @@ def tile_list_tabw_bias_kernel(tc, tab, w, b, offs, out):
                 nc.scalar.activation(results[i][:], accs[i][:], IDENTITY, bias=bias[:])
             queue.dma_start(out[:, j0:j1], results[i][:])
 
-        nc.vector.memset(scales[64:P, :], 0)
-        nc.vector.memset(scales[32:64, :], 0)
+        nc.vector.memset(scales[:], 0)
         nc.vector.memset(planes[:], 0)
-        load_scales(0)
-        load_scales(1)
         nc.sync.dma_start(offsets[:], offs)
-        load_scales(2)
+        nc.scalar.dma_start(bias[:], b.rearrange("(n one) -> n one", one=1))
         load_w(1)
+        for a in range(PASSES):
+            load_scales(a)
         load_w(2)
         load_words(0)
         load_words(1)
@@ -145,7 +145,6 @@ def tile_list_tabw_bias_kernel(tc, tab, w, b, offs, out):
         load_w(0)
         place_scales(0)
         place_scales(2)
-        nc.sync.dma_start(bias[:], b.rearrange("(n one) -> n one", one=1))
 
         for a in (0, 1):
             pick_words(picked[a][:], a, 0, S)

@@ -28,28 +28,25 @@ def tile_list_tabw_bias_kernel(tc, tab, w, b, offs, out):
         tc.tile_pool(name="lists", bufs=1) as lists,
         tc.tile_pool(name="keep", bufs=1) as keep,
         tc.tile_pool(name="late", bufs=1) as late,
-        tc.tile_pool(name="last", bufs=1) as last,
         tc.psum_pool(name="psum", bufs=1) as psum,
     ):
         offsets = lists.tile([P, S // 16], U16, name="offsets")
-        scales = late.tile([P, T // 4], I32, name="scales", align_bytes=64, offset=0)
-        w_raw = [late.tile([P, 4, M], F32, name="w_raw0", align_bytes=64, offset=0)] + [
+        scales = late.tile([P, T // 4], I32, name="scales", align_bytes=64, offset=4 * THIRD)
+        w_raw = [late.tile([P, 4, M], F32, name="w_raw0", align_bytes=64, offset=2 * THIRD)] + [
             keep.tile([P, 4, M], F32, name=f"w_raw{a}", align_bytes=64) for a in (1, 2)
         ]
         bias = keep.tile([P, 1], F32, name="bias")
         words = [keep.tile([P, T], I32, name=f"words{a}", align_bytes=64) for a in (0, 1)] + [
-            late.tile([P, T], I32, name="words2", align_bytes=64, offset=16 * M)
+            late.tile([P, T], I32, name="words2", align_bytes=64, offset=8 * THIRD)
         ]
         picked_rows = keep.tile([P, S // 4], I32, name="picked_rows", align_bytes=64)
-        planes = keep.tile([P, PASSES * S // 4], I32, name="planes", align_bytes=64)
+        planes = [keep.tile([P, S // 4], I32, name=f"planes{a}", align_bytes=64) for a in range(PASSES)]
         picked = [keep.tile([P, S], U32, name=f"picked{a}", align_bytes=64) for a in (0, 1)]
         w_bf_early = keep.tile([P, 2, M, 4], BF16, name="w_bf_early", align_bytes=64)
-        w_bf_late = last.tile(
-            [P, M, 4], BF16, name="w_bf_late", align_bytes=64, offset=8 * THIRD - 4 * M
-        )
-        picked_last = [
-            last.tile([P, THIRD], U32, name=f"picked_last{i}", align_bytes=64, offset=4 * THIRD * i)
-            for i in range(3)
+        w_bf_late = keep.tile([P, M, 4], BF16, name="w_bf_late", align_bytes=64)
+        picked_last = [keep.tile([P, THIRD], U32, name="picked_last0", align_bytes=64)] + [
+            late.tile([P, THIRD], U32, name=f"picked_last{i}", align_bytes=64, offset=4 * THIRD * (i - 1))
+            for i in (1, 2)
         ]
         w_codes = keep.tile([P, PASSES * M], U32, name="w_codes", align_bytes=64)
         w_scales = keep.tile([P, PASSES * M], U8, name="w_scales", align_bytes=64)
@@ -85,20 +82,18 @@ def tile_list_tabw_bias_kernel(tc, tab, w, b, offs, out):
                 in_=src,
             )
 
-        def place_scales(a):
-            for quad in range(4):
-                src = ROW_BASE[a] + 4 * ROW_STEP * quad
-                dst = 32 * quad + 4 * a
-                nc.sync.dma_start(
-                    planes[dst : dst + 4, a * S // 4 : (a + 1) * S // 4],
-                    picked_rows[src : src + 4 * ROW_STEP : ROW_STEP, :],
-                )
+        def place_scales(a, r):
+            src = ROW_BASE[a] + ROW_STEP * r
+            nc.sync.dma_start(
+                planes[a][4 * a + r : P : 32, :],
+                picked_rows[src : src + 16 * ROW_STEP : 4 * ROW_STEP, :],
+            )
 
         pieces = [(0, 512), (512, 1024), (1024, 1280), (1280, 1536)]
         accs = [psum.tile([M, j1 - j0], F32, name=f"acc{j0}") for j0, j1 in pieces]
         results = [keep.tile([M, j1 - j0], F32, name=f"result{j0}") for j0, j1 in pieces]
 
-        def multiply(a, i):
+        def multiply(a, i, stop=False):
             j0, j1 = pieces[i]
             if a < 2:
                 codes = picked[a][:, j0:j1]
@@ -110,9 +105,9 @@ def tile_list_tabw_bias_kernel(tc, tab, w, b, offs, out):
                 lhsT=w_codes[:, M * a : M * (a + 1)].bitcast(FP8X4),
                 lhsT_scale=w_scales[:, M * a : M * (a + 1)],
                 rhs=codes.bitcast(FP8X4),
-                rhs_scale=planes[:].bitcast(U8)[4 * a : P, a * S + j0 : a * S + j1],
+                rhs_scale=planes[a][:].bitcast(U8)[4 * a : P, j0:j1],
                 start=(a == 1),
-                stop=(a == 2),
+                stop=stop,
             )
 
         def finish(i, on_vector, queue):
@@ -124,7 +119,8 @@ def tile_list_tabw_bias_kernel(tc, tab, w, b, offs, out):
             queue.dma_start(out[:, j0:j1], results[i][:])
 
         nc.vector.memset(scales[:], 0)
-        nc.vector.memset(planes[:], 0)
+        for a in range(PASSES):
+            nc.vector.memset(planes[a][:], 0)
         nc.sync.dma_start(offsets[:], offs)
         nc.scalar.dma_start(bias[:], b.rearrange("(n one) -> n one", one=1))
         load_w(1)
@@ -140,30 +136,37 @@ def tile_list_tabw_bias_kernel(tc, tab, w, b, offs, out):
         for a in (1, 2):
             round_w(w_bf_early[:, a - 1], a)
         quantise_w(w_bf_early[:].rearrange("p a n j -> p (a n j)"), 1, 3)
-        place_scales(1)
+        for r in (0, 1):
+            place_scales(1, r)
+            place_scales(2, r)
+        for r in (2, 3):
+            place_scales(1, r)
         load_words(2)
         load_w(0)
-        place_scales(0)
-        place_scales(2)
+        for r in (2, 3):
+            place_scales(2, r)
+            place_scales(0, r)
+        for r in (0, 1):
+            place_scales(0, r)
 
         for a in (0, 1):
             pick_words(picked[a][:], a, 0, S)
         for i in range(len(pieces)):
             multiply(1, i)
         pick_words(picked_last[0][:], 2, 0, THIRD)
+        multiply(2, 0)
         round_w(w_bf_late[:], 0)
         quantise_w(w_bf_late[:].rearrange("p n j -> p (n j)"), 0, 1)
-        multiply(0, 0)
-        multiply(2, 0)
+        multiply(0, 0, stop=True)
         finish(0, False, nc.sync)
         pick_words(picked_last[1][:], 2, THIRD, 2 * THIRD)
         multiply(0, 1)
-        multiply(2, 1)
+        multiply(2, 1, stop=True)
         finish(1, False, nc.sync)
         multiply(0, 2)
         multiply(0, 3)
         pick_words(picked_last[2][:], 2, 2 * THIRD, S)
-        multiply(2, 2)
-        multiply(2, 3)
+        multiply(2, 2, stop=True)
+        multiply(2, 3, stop=True)
         finish(2, False, nc.scalar)
         finish(3, True, nc.sync)

@@ -32,9 +32,11 @@ def tile_list_tabw_bias_kernel(tc, tab, w, b, offs, out):
     ):
         offsets = lists.tile([P, S // 16], U16, name="offsets")
         scales = late.tile([P, T // 4], I32, name="scales", align_bytes=64, offset=4 * THIRD)
-        w_raw = [late.tile([P, 4, M], F32, name="w_raw0", align_bytes=64, offset=2 * THIRD)] + [
-            keep.tile([P, 4, M], F32, name=f"w_raw{a}", align_bytes=64) for a in (1, 2)
+        w_half = [
+            late.tile([P, 2, M], F32, name="w_half0", align_bytes=64, offset=5 * THIRD),
+            late.tile([P, 2, M], F32, name="w_half1", align_bytes=64, offset=3 * THIRD),
         ]
+        w_raw = {a: keep.tile([P, 4, M], F32, name=f"w_raw{a}", align_bytes=64) for a in (1, 2)}
         bias = keep.tile([P, 1], F32, name="bias")
         words = [keep.tile([P, T], I32, name=f"words{a}", align_bytes=64) for a in (0, 1)] + [
             late.tile([P, T], I32, name="words2", align_bytes=64, offset=8 * THIRD)
@@ -82,9 +84,9 @@ def tile_list_tabw_bias_kernel(tc, tab, w, b, offs, out):
                 in_=src,
             )
 
-        def place_scales(a, r):
+        def place_scales(a, r, queue=nc.sync):
             src = ROW_BASE[a] + ROW_STEP * r
-            nc.sync.dma_start(
+            queue.dma_start(
                 planes[a][4 * a + r : P : 32, :],
                 picked_rows[src : src + 16 * ROW_STEP : 4 * ROW_STEP, :],
             )
@@ -136,18 +138,17 @@ def tile_list_tabw_bias_kernel(tc, tab, w, b, offs, out):
         for a in (1, 2):
             round_w(w_bf_early[:, a - 1], a)
         quantise_w(w_bf_early[:].rearrange("p a n j -> p (a n j)"), 1, 3)
-        for r in (0, 1):
+        for r in range(4):
             place_scales(1, r)
-            place_scales(2, r)
-        for r in (2, 3):
-            place_scales(1, r)
+        for r in (0, 1, 2):
+            place_scales(0, r, nc.gpsimd)
         load_words(2)
-        load_w(0)
-        for r in (2, 3):
+        w0_rows = w[0:512, :].rearrange("(p j) n -> p j n", j=4)
+        for half in (0, 1):
+            nc.sync.dma_start(w_half[half][:], w0_rows[:, 2 * half : 2 * half + 2, :])
+        for r in range(4):
             place_scales(2, r)
-            place_scales(0, r)
-        for r in (0, 1):
-            place_scales(0, r)
+        place_scales(0, 3)
 
         for a in (0, 1):
             pick_words(picked[a][:], a, 0, S)
@@ -155,7 +156,10 @@ def tile_list_tabw_bias_kernel(tc, tab, w, b, offs, out):
             multiply(1, i)
         pick_words(picked_last[0][:], 2, 0, THIRD)
         multiply(2, 0)
-        round_w(w_bf_late[:], 0)
+        for half in (0, 1):
+            nc.scalar.copy(
+                w_bf_late[:, :, 2 * half : 2 * half + 2], w_half[half][:].rearrange("p j n -> p n j")
+            )
         quantise_w(w_bf_late[:].rearrange("p n j -> p (n j)"), 0, 1)
         multiply(0, 0, stop=True)
         finish(0, False, nc.sync)

@@ -16,10 +16,19 @@ ADD = mybir.AluOpType.add
 P = 128
 PASSES = K // 512
 
-
-ROW_BASE = (32, 33, 34)
+ROW_BASE = 32
 ROW_STEP = 4
+
 THIRD = S // 3
+PIECE = THIRD // 2
+PIECES = S // PIECE
+SLIVER = T // 8
+
+OVERLAP = 64
+AT_THIRDS = 4 * S
+AT_SCALES = AT_THIRDS - OVERLAP
+AT_WORDS2 = AT_THIRDS + 2 * 4 * THIRD
+SCALES_BYTES = AT_WORDS2 + OVERLAP - AT_SCALES
 
 
 def tile_list_tabw_bias_kernel(tc, tab, w, b, offs, out):
@@ -27,150 +36,147 @@ def tile_list_tabw_bias_kernel(tc, tab, w, b, offs, out):
     with (
         tc.tile_pool(name="lists", bufs=1) as lists,
         tc.tile_pool(name="keep", bufs=1) as keep,
-        tc.tile_pool(name="late", bufs=1) as late,
+        tc.tile_pool(name="shared", bufs=1) as shared,
         tc.psum_pool(name="psum", bufs=1) as psum,
     ):
         offsets = lists.tile([P, S // 16], U16, name="offsets")
-        scales = late.tile([P, T // 4], I32, name="scales", align_bytes=64, offset=4 * THIRD)
-        w_half = [
-            late.tile([P, 2, M], F32, name="w_half0", align_bytes=64, offset=5 * THIRD),
-            late.tile([P, 2, M], F32, name="w_half1", align_bytes=64, offset=3 * THIRD),
-        ]
-        w_raw = {a: keep.tile([P, 4, M], F32, name=f"w_raw{a}", align_bytes=64) for a in (1, 2)}
         bias = keep.tile([P, 1], F32, name="bias")
-        words = [keep.tile([P, T], I32, name=f"words{a}", align_bytes=64) for a in (0, 1)] + [
-            late.tile([P, T], I32, name="words2", align_bytes=64, offset=8 * THIRD)
+
+        scales = shared.tile([P, SCALES_BYTES // 4], I32, name="scales", align_bytes=64, offset=AT_SCALES)
+        scale_window = scales[:, 0 : T // 4]
+        words = [
+            keep.tile([P, T], I32, name="words0", align_bytes=64),
+            keep.tile([P, T], I32, name="words1", align_bytes=64),
+            shared.tile([P, T], I32, name="words2", align_bytes=64, offset=AT_WORDS2),
+        ]
+        picked = [
+            shared.tile([P, S], U32, name="picked0", align_bytes=64, offset=0),
+            keep.tile([P, S], U32, name="picked1", align_bytes=64),
+        ]
+        w_raw = [
+            shared.tile([P, 4, M], F32, name="w_raw0", align_bytes=64, offset=AT_THIRDS),
+            keep.tile([P, 4, M], F32, name="w_raw1", align_bytes=64),
+            shared.tile([P, 4, M], F32, name="w_raw2", align_bytes=64, offset=AT_THIRDS + 4 * THIRD),
+        ]
+        picked_thirds = [
+            keep.tile([P, THIRD], U32, name="third0", align_bytes=64),
+            shared.tile([P, THIRD], U32, name="third1", align_bytes=64, offset=AT_THIRDS),
+            shared.tile([P, THIRD], U32, name="third2", align_bytes=64, offset=AT_THIRDS + 4 * THIRD),
         ]
         picked_rows = keep.tile([P, S // 4], I32, name="picked_rows", align_bytes=64)
-        planes = [keep.tile([P, S // 4], I32, name=f"planes{a}", align_bytes=64) for a in range(PASSES)]
-        picked = [keep.tile([P, S], U32, name=f"picked{a}", align_bytes=64) for a in (0, 1)]
-        w_bf_early = keep.tile([P, 2, M, 4], BF16, name="w_bf_early", align_bytes=64)
-        w_bf_late = keep.tile([P, M, 4], BF16, name="w_bf_late", align_bytes=64)
-        picked_last = [keep.tile([P, THIRD], U32, name="picked_last0", align_bytes=64)] + [
-            late.tile([P, THIRD], U32, name=f"picked_last{i}", align_bytes=64, offset=4 * THIRD * (i - 1))
-            for i in (1, 2)
-        ]
+        planes = [keep.tile([P, S // 4], I32, name=f"plane{a}", align_bytes=64) for a in range(PASSES)]
+        w_bf = [keep.tile([P, M, 4], BF16, name=f"w_bf{a}", align_bytes=64) for a in range(PASSES)]
         w_codes = keep.tile([P, PASSES * M], U32, name="w_codes", align_bytes=64)
         w_scales = keep.tile([P, PASSES * M], U8, name="w_scales", align_bytes=64)
-
-        scale_rows = tab[:, 512 * T : 528 * T].bitcast(I32).rearrange("a (q t) -> a q t", q=16)
+        accs = [psum.tile([M, PIECE], F32, name=f"acc{i}") for i in range(PIECES)]
+        results = [keep.tile([M, PIECE], F32, name=f"result{i}") for i in range(PIECES)]
 
         def load_scales(a):
-            nc.sync.dma_start(scales[ROW_BASE[a] : ROW_BASE[a] + 16 * ROW_STEP : ROW_STEP, :], scale_rows[a])
+            rows = tab[a, 512 * T : 528 * T].bitcast(I32).rearrange("(q t) -> q t", q=16)
+            first = ROW_BASE + a
+            nc.sync.dma_start(scales[first : first + 16 * ROW_STEP : ROW_STEP, 0 : T // 4], rows)
 
-        def load_words(a):
-            nc.sync.dma_start(
-                words[a][:],
-                tab[a, 0 : 512 * T].bitcast(I32).rearrange("(p t) -> p t", p=P),
-            )
+        def load_words(a, t0, t1):
+            table = tab[a, 0 : 512 * T].bitcast(I32).rearrange("(p t) -> p t", p=P)
+            nc.sync.dma_start(words[a][:, t0:t1], table[:, t0:t1])
 
         def load_w(a):
+            rows = w[512 * a : 512 * (a + 1), :].rearrange("(p t) n -> p t n", t=4)
+            nc.sync.dma_start(w_raw[a][:], rows)
+
+        def carry_rows(a, r):
+            first = ROW_BASE + a + ROW_STEP * r
             nc.sync.dma_start(
-                w_raw[a][:], w[512 * a : 512 * (a + 1), :].rearrange("(p j) n -> p j n", j=4)
+                planes[a][4 * a + r : P : 32, :],
+                picked_rows[first : first + 16 * ROW_STEP : 4 * ROW_STEP, :],
             )
 
         def pick_words(dst, a, j0, j1):
-            nc.vector.tensor_copy(
-                dst, words[a][:].bitcast(U32).indirect(offsets[:, j0 // 16 : j1 // 16])
+            nc.vector.tensor_copy(dst, words[a][:].bitcast(U32).indirect(offsets[:, j0 // 16 : j1 // 16]))
+
+        def quantise_w(a):
+            nc.scalar.copy(
+                w_bf[a][:].rearrange("p (c i) t -> p c t i", i=4),
+                w_raw[a][:].rearrange("p t (c i) -> p c t i", i=4),
             )
-
-        def round_w(dst, a):
-            nc.scalar.copy(dst, w_raw[a][:].rearrange("p j n -> p n j"))
-
-        def quantise_w(src, a0, a1):
             nc.vector.quantize_mx(
-                out=w_codes[:, M * a0 : M * a1].bitcast(FP8X4),
-                scales=w_scales[:, M * a0 : M * a1],
-                in_=src,
+                out=w_codes[:, M * a : M * (a + 1)].bitcast(FP8X4),
+                scales=w_scales[:, M * a : M * (a + 1)],
+                in_=w_bf[a][:].rearrange("p n t -> p (n t)"),
             )
 
-        def place_scales(a, r, queue=nc.sync):
-            src = ROW_BASE[a] + ROW_STEP * r
-            queue.dma_start(
-                planes[a][4 * a + r : P : 32, :],
-                picked_rows[src : src + 16 * ROW_STEP : 4 * ROW_STEP, :],
-            )
-
-        pieces = [(0, 512), (512, 1024), (1024, 1280), (1280, 1536)]
-        accs = [psum.tile([M, j1 - j0], F32, name=f"acc{j0}") for j0, j1 in pieces]
-        results = [keep.tile([M, j1 - j0], F32, name=f"result{j0}") for j0, j1 in pieces]
-
-        def multiply(a, i, stop=False):
-            j0, j1 = pieces[i]
-            if a < 2:
-                codes = picked[a][:, j0:j1]
+        def multiply(a, i):
+            j0 = PIECE * i
+            if a == 2:
+                codes = picked_thirds[j0 // THIRD][:, j0 % THIRD : j0 % THIRD + PIECE]
             else:
-                third = j0 // THIRD
-                codes = picked_last[third][:, j0 - third * THIRD : j1 - third * THIRD]
+                codes = picked[a][:, j0 : j0 + PIECE]
             nc.tensor.matmul_mx(
                 out=accs[i][:],
                 lhsT=w_codes[:, M * a : M * (a + 1)].bitcast(FP8X4),
                 lhsT_scale=w_scales[:, M * a : M * (a + 1)],
                 rhs=codes.bitcast(FP8X4),
-                rhs_scale=planes[a][:].bitcast(U8)[4 * a : P, j0:j1],
+                rhs_scale=planes[a][:].bitcast(U8)[4 * a : P, j0 : j0 + PIECE],
                 start=(a == 1),
-                stop=stop,
+                stop=(a == 2),
             )
 
-        def finish(i, on_vector, queue):
-            j0, j1 = pieces[i]
-            if on_vector:
-                nc.vector.tensor_scalar(results[i][:], accs[i][:], bias[:], None, op0=ADD)
-            else:
-                nc.scalar.activation(results[i][:], accs[i][:], IDENTITY, bias=bias[:])
-            queue.dma_start(out[:, j0:j1], results[i][:])
+        def add_bias_on_scalar(i):
+            nc.scalar.activation(results[i][:], accs[i][:], IDENTITY, bias=bias[:])
 
-        nc.vector.memset(scales[:], 0)
+        def store(i, queue):
+            queue.dma_start(out[:, PIECE * i : PIECE * (i + 1)], results[i][:])
+
+        nc.vector.memset(scale_window, 0)
         for a in range(PASSES):
             nc.vector.memset(planes[a][:], 0)
+
         nc.sync.dma_start(offsets[:], offs)
         nc.scalar.dma_start(bias[:], b.rearrange("(n one) -> n one", one=1))
         load_w(1)
+        load_words(0, 0, SLIVER)
         for a in range(PASSES):
             load_scales(a)
-        load_w(2)
-        load_words(0)
-        load_words(1)
+        load_words(0, SLIVER, T)
+        load_words(1, 0, T)
 
-        nc.vector.tensor_copy(
-            picked_rows[:].bitcast(U8), scales[:].bitcast(U8).indirect(offsets[:])
-        )
-        for a in (1, 2):
-            round_w(w_bf_early[:, a - 1], a)
-        quantise_w(w_bf_early[:].rearrange("p a n j -> p (a n j)"), 1, 3)
+        nc.vector.tensor_copy(picked_rows[:].bitcast(U8), scale_window.bitcast(U8).indirect(offsets[:]))
+        quantise_w(1)
+
+        for r in range(3):
+            carry_rows(1, r)
+            carry_rows(0, r)
+        load_words(2, 0, T - SLIVER)
+        carry_rows(1, 3)
+        load_words(2, T - SLIVER, T)
+        load_w(0)
+        load_w(2)
+        carry_rows(0, 3)
         for r in range(4):
-            place_scales(1, r)
-        for r in (0, 1, 2):
-            place_scales(0, r, nc.gpsimd)
-        load_words(2)
-        w0_rows = w[0:512, :].rearrange("(p j) n -> p j n", j=4)
-        for half in (0, 1):
-            nc.sync.dma_start(w_half[half][:], w0_rows[:, 2 * half : 2 * half + 2, :])
-        for r in range(4):
-            place_scales(2, r)
-        place_scales(0, 3)
+            carry_rows(2, r)
 
         for a in (0, 1):
             pick_words(picked[a][:], a, 0, S)
-        for i in range(len(pieces)):
+        for i in range(PIECES):
             multiply(1, i)
-        pick_words(picked_last[0][:], 2, 0, THIRD)
-        multiply(2, 0)
-        for half in (0, 1):
-            nc.scalar.copy(
-                w_bf_late[:, :, 2 * half : 2 * half + 2], w_half[half][:].rearrange("p j n -> p n j")
-            )
-        quantise_w(w_bf_late[:].rearrange("p n j -> p (n j)"), 0, 1)
-        multiply(0, 0, stop=True)
-        finish(0, False, nc.sync)
-        pick_words(picked_last[1][:], 2, THIRD, 2 * THIRD)
-        multiply(0, 1)
-        multiply(2, 1, stop=True)
-        finish(1, False, nc.sync)
-        multiply(0, 2)
-        multiply(0, 3)
-        pick_words(picked_last[2][:], 2, 2 * THIRD, S)
-        multiply(2, 2, stop=True)
-        multiply(2, 3, stop=True)
-        finish(2, False, nc.scalar)
-        finish(3, True, nc.sync)
+
+        pick_words(picked_thirds[0][:], 2, 0, THIRD)
+        quantise_w(0)
+        for i in range(PIECES):
+            multiply(0, i)
+
+        pick_words(picked_thirds[1][:], 2, THIRD, 2 * THIRD)
+        quantise_w(2)
+        for i in range(PIECES - 2):
+            multiply(2, i)
+            add_bias_on_scalar(i)
+            store(i, nc.sync)
+
+        pick_words(picked_thirds[2][:], 2, 2 * THIRD, S)
+        on_scalar, on_vector = PIECES - 2, PIECES - 1
+        multiply(2, on_scalar)
+        multiply(2, on_vector)
+        add_bias_on_scalar(on_scalar)
+        store(on_scalar, nc.scalar)
+        nc.vector.tensor_scalar(results[on_vector][:], accs[on_vector][:], bias[:], None, op0=ADD)
+        store(on_vector, nc.sync)

@@ -22,7 +22,7 @@ ROW_STEP = 4
 THIRD = S // 3
 PIECE = THIRD // 2
 PIECES = S // PIECE
-SLIVER = T // 8
+SLIVER = T // 4
 
 OVERLAP = 64
 AT_THIRDS = 4 * S
@@ -54,18 +54,19 @@ def tile_list_tabw_bias_kernel(tc, tab, w, b, offs, out):
             keep.tile([P, S], U32, name="picked1", align_bytes=64),
         ]
         w_raw = [
-            shared.tile([P, 4, M], F32, name="w_raw0", align_bytes=64, offset=AT_THIRDS),
-            keep.tile([P, 4, M], F32, name="w_raw1", align_bytes=64),
+            keep.tile([P, 4, M], F32, name="w_raw0", align_bytes=64),
+            shared.tile([P, 4, M], F32, name="w_raw1", align_bytes=64, offset=AT_THIRDS),
             shared.tile([P, 4, M], F32, name="w_raw2", align_bytes=64, offset=AT_THIRDS + 4 * THIRD),
         ]
         picked_thirds = [
             keep.tile([P, THIRD], U32, name="third0", align_bytes=64),
-            shared.tile([P, THIRD], U32, name="third1", align_bytes=64, offset=AT_THIRDS),
+            keep.tile([P, THIRD], U32, name="third1", align_bytes=64),
             shared.tile([P, THIRD], U32, name="third2", align_bytes=64, offset=AT_THIRDS + 4 * THIRD),
         ]
         picked_rows = keep.tile([P, S // 4], I32, name="picked_rows", align_bytes=64)
         planes = [keep.tile([P, S // 4], I32, name=f"plane{a}", align_bytes=64) for a in range(PASSES)]
-        w_bf = [keep.tile([P, M, 4], BF16, name=f"w_bf{a}", align_bytes=64) for a in range(PASSES)]
+        w_bf_early = keep.tile([P, M, 4], BF16, name="w_bf_early", align_bytes=64)
+        w_bf_late = keep.tile([P, 2, M, 4], BF16, name="w_bf_late", align_bytes=64)
         w_codes = keep.tile([P, PASSES * M], U32, name="w_codes", align_bytes=64)
         w_scales = keep.tile([P, PASSES * M], U8, name="w_scales", align_bytes=64)
         accs = [psum.tile([M, PIECE], F32, name=f"acc{i}") for i in range(PIECES)]
@@ -79,6 +80,7 @@ def tile_list_tabw_bias_kernel(tc, tab, w, b, offs, out):
         def load_words(a, t0, t1):
             table = tab[a, 0 : 512 * T].bitcast(I32).rearrange("(p t) -> p t", p=P)
             nc.sync.dma_start(words[a][:, t0:t1], table[:, t0:t1])
+
 
         def load_w(a):
             rows = w[512 * a : 512 * (a + 1), :].rearrange("(p t) n -> p t n", t=4)
@@ -94,15 +96,17 @@ def tile_list_tabw_bias_kernel(tc, tab, w, b, offs, out):
         def pick_words(dst, a, j0, j1):
             nc.vector.tensor_copy(dst, words[a][:].bitcast(U32).indirect(offsets[:, j0 // 16 : j1 // 16]))
 
-        def quantise_w(a):
+        def round_w(dst, src):
             nc.scalar.copy(
-                w_bf[a][:].rearrange("p (c i) t -> p c t i", i=4),
-                w_raw[a][:].rearrange("p t (c i) -> p c t i", i=4),
+                dst.rearrange("p (c i) t -> p c t i", i=4),
+                src.rearrange("p t (c i) -> p c t i", i=4),
             )
+
+        def quantise(a0, a1, rounded):
             nc.vector.quantize_mx(
-                out=w_codes[:, M * a : M * (a + 1)].bitcast(FP8X4),
-                scales=w_scales[:, M * a : M * (a + 1)],
-                in_=w_bf[a][:].rearrange("p n t -> p (n t)"),
+                out=w_codes[:, M * a0 : M * a1].bitcast(FP8X4),
+                scales=w_scales[:, M * a0 : M * a1],
+                in_=rounded,
             )
 
         def multiply(a, i):
@@ -117,7 +121,7 @@ def tile_list_tabw_bias_kernel(tc, tab, w, b, offs, out):
                 lhsT_scale=w_scales[:, M * a : M * (a + 1)],
                 rhs=codes.bitcast(FP8X4),
                 rhs_scale=planes[a][:].bitcast(U8)[4 * a : P, j0 : j0 + PIECE],
-                start=(a == 1),
+                start=(a == 0),
                 stop=(a == 2),
             )
 
@@ -133,50 +137,48 @@ def tile_list_tabw_bias_kernel(tc, tab, w, b, offs, out):
 
         nc.sync.dma_start(offsets[:], offs)
         nc.scalar.dma_start(bias[:], b.rearrange("(n one) -> n one", one=1))
-        load_w(1)
         load_words(0, 0, SLIVER)
         for a in range(PASSES):
             load_scales(a)
         load_words(0, SLIVER, T)
+        load_w(0)
         load_words(1, 0, T)
 
         nc.vector.tensor_copy(picked_rows[:].bitcast(U8), scale_window.bitcast(U8).indirect(offsets[:]))
-        quantise_w(1)
 
-        for r in range(3):
-            carry_rows(1, r)
-            carry_rows(0, r)
-        load_words(2, 0, T - SLIVER)
-        carry_rows(1, 3)
-        load_words(2, T - SLIVER, T)
-        load_w(0)
+        carries = [(a, r) for a in (0, 2, 1) for r in range(4)]
+        carry_rows(*carries[0])
+        load_words(2, 0, T)
+        for a, r in carries[1:6]:
+            carry_rows(a, r)
+        load_w(1)
         load_w(2)
-        carry_rows(0, 3)
-        for r in range(4):
-            carry_rows(2, r)
+        for a, r in carries[6:]:
+            carry_rows(a, r)
 
-        for a in (0, 1):
-            pick_words(picked[a][:], a, 0, S)
-        for i in range(PIECES):
-            multiply(1, i)
-
-        pick_words(picked_thirds[0][:], 2, 0, THIRD)
-        quantise_w(0)
+        pick_words(picked[0][:], 0, 0, S)
+        round_w(w_bf_early[:], w_raw[0][:])
+        quantise(0, 1, w_bf_early[:].rearrange("p n t -> p (n t)"))
+        pick_words(picked[1][:], 1, 0, S)
         for i in range(PIECES):
             multiply(0, i)
 
+        pick_words(picked_thirds[0][:], 2, 0, THIRD)
         pick_words(picked_thirds[1][:], 2, THIRD, 2 * THIRD)
-        quantise_w(2)
-        for i in range(PIECES - 2):
-            multiply(2, i)
-            add_bias_on_scalar(i)
-            store(i, nc.sync)
-
+        for a in (1, 2):
+            round_w(w_bf_late[:, a - 1], w_raw[a][:])
+        quantise(1, 3, w_bf_late[:].rearrange("p a n t -> p (a n t)"))
         pick_words(picked_thirds[2][:], 2, 2 * THIRD, S)
-        on_scalar, on_vector = PIECES - 2, PIECES - 1
-        multiply(2, on_scalar)
-        multiply(2, on_vector)
-        add_bias_on_scalar(on_scalar)
-        store(on_scalar, nc.scalar)
-        nc.vector.tensor_scalar(results[on_vector][:], accs[on_vector][:], bias[:], None, op0=ADD)
-        store(on_vector, nc.sync)
+        for i in range(PIECES - 2):
+            multiply(1, i)
+            multiply(2, i)
+        for i in range(PIECES - 2, PIECES):
+            multiply(1, i)
+        for i in range(PIECES - 2, PIECES):
+            multiply(2, i)
+        for i in range(PIECES):
+            if i in (3, 5):
+                nc.vector.tensor_scalar(results[i][:], accs[i][:], bias[:], None, op0=ADD)
+            else:
+                add_bias_on_scalar(i)
+            store(i, nc.scalar if i == 4 else nc.sync)

@@ -21,7 +21,8 @@ ROW_STEP = 4
 
 THIRD = S // 3
 PIECE = THIRD // 2
-PIECES = S // PIECE
+EDGES = [0, PIECE // 2] + list(range(PIECE, S + 1, PIECE))
+PIECES = len(EDGES) - 1
 SLIVER = T // 4
 
 OVERLAP = 64
@@ -40,7 +41,9 @@ def tile_list_tabw_bias_kernel(tc, tab, w, b, offs, out):
         tc.psum_pool(name="psum", bufs=1) as psum,
     ):
         offsets = lists.tile([P, S // 16], U16, name="offsets")
-        bias = keep.tile([P, 1], F32, name="bias")
+        bias_rows = keep.tile([P, 32], F32, name="bias_rows", align_bytes=64)
+        bias_cols = keep.tile([P, 32], F32, name="bias_cols", align_bytes=64)
+        bias = bias_cols[:, 0:1]
 
         scales = shared.tile([P, SCALES_BYTES // 4], I32, name="scales", align_bytes=64, offset=AT_SCALES)
         scale_window = scales[:, 0 : T // 4]
@@ -69,8 +72,8 @@ def tile_list_tabw_bias_kernel(tc, tab, w, b, offs, out):
         w_bf_late = keep.tile([P, 2, M, 4], BF16, name="w_bf_late", align_bytes=64)
         w_codes = keep.tile([P, PASSES * M], U32, name="w_codes", align_bytes=64)
         w_scales = keep.tile([P, PASSES * M], U8, name="w_scales", align_bytes=64)
-        accs = [psum.tile([M, PIECE], F32, name=f"acc{i}") for i in range(PIECES)]
-        results = [keep.tile([M, PIECE], F32, name=f"result{i}") for i in range(PIECES)]
+        accs = [psum.tile([M, EDGES[i + 1] - EDGES[i]], F32, name=f"acc{i}") for i in range(PIECES)]
+        results = [keep.tile([M, EDGES[i + 1] - EDGES[i]], F32, name=f"result{i}") for i in range(PIECES)]
 
         def load_scales(a):
             rows = tab[a, 512 * T : 528 * T].bitcast(I32).rearrange("(q t) -> q t", q=16)
@@ -110,33 +113,35 @@ def tile_list_tabw_bias_kernel(tc, tab, w, b, offs, out):
             )
 
         def multiply(a, i):
-            j0 = PIECE * i
+            j0, width = EDGES[i], EDGES[i + 1] - EDGES[i]
             if a == 2:
-                codes = picked_thirds[j0 // THIRD][:, j0 % THIRD : j0 % THIRD + PIECE]
+                codes = picked_thirds[j0 // THIRD][:, j0 % THIRD : j0 % THIRD + width]
             else:
-                codes = picked[a][:, j0 : j0 + PIECE]
+                codes = picked[a][:, j0 : j0 + width]
             nc.tensor.matmul_mx(
                 out=accs[i][:],
                 lhsT=w_codes[:, M * a : M * (a + 1)].bitcast(FP8X4),
                 lhsT_scale=w_scales[:, M * a : M * (a + 1)],
                 rhs=codes.bitcast(FP8X4),
-                rhs_scale=planes[a][:].bitcast(U8)[4 * a : P, j0 : j0 + PIECE],
+                rhs_scale=planes[a][:].bitcast(U8)[4 * a : P, j0 : j0 + width],
                 start=(a == 0),
                 stop=(a == 2),
             )
 
         def add_bias_on_scalar(i):
-            nc.scalar.activation(results[i][:], accs[i][:], IDENTITY, bias=bias[:])
+            nc.scalar.activation(results[i][:], accs[i][:], IDENTITY, bias=bias)
 
         def store(i, queue):
-            queue.dma_start(out[:, PIECE * i : PIECE * (i + 1)], results[i][:])
+            queue.dma_start(out[:, EDGES[i] : EDGES[i + 1]], results[i][:])
 
         nc.vector.memset(scale_window, 0)
         for a in range(PASSES):
             nc.vector.memset(planes[a][:], 0)
 
         nc.sync.dma_start(offsets[:], offs)
-        nc.scalar.dma_start(bias[:], b.rearrange("(n one) -> n one", one=1))
+        nc.gpsimd.memset(bias_rows[:], 0.0)
+        nc.scalar.dma_start(bias_rows[0:P:32, :], b.rearrange("(q i) -> q i", i=32))
+        nc.vector.transpose(bias_cols[:], bias_rows[:])
         load_words(0, 0, SLIVER)
         for a in range(PASSES):
             load_scales(a)
@@ -146,15 +151,16 @@ def tile_list_tabw_bias_kernel(tc, tab, w, b, offs, out):
 
         nc.vector.tensor_copy(picked_rows[:].bitcast(U8), scale_window.bitcast(U8).indirect(offsets[:]))
 
-        carries = [(a, r) for a in (0, 2, 1) for r in range(4)]
-        carry_rows(*carries[0])
+        for a in range(PASSES):
+            carry_rows(a, 0)
         load_words(2, 0, T)
-        for a, r in carries[1:6]:
-            carry_rows(a, r)
+        for r in range(1, 4):
+            carry_rows(0, r)
         load_w(1)
         load_w(2)
-        for a, r in carries[6:]:
-            carry_rows(a, r)
+        for a in (2, 1):
+            for r in range(1, 4):
+                carry_rows(a, r)
 
         pick_words(picked[0][:], 0, 0, S)
         round_w(w_bf_early[:], w_raw[0][:])
@@ -167,7 +173,8 @@ def tile_list_tabw_bias_kernel(tc, tab, w, b, offs, out):
         pick_words(picked_thirds[1][:], 2, THIRD, 2 * THIRD)
         for a in (1, 2):
             round_w(w_bf_late[:, a - 1], w_raw[a][:])
-        quantise(1, 3, w_bf_late[:].rearrange("p a n t -> p (a n t)"))
+        for a in (1, 2):
+            quantise(a, a + 1, w_bf_late[:, a - 1].rearrange("p n t -> p (n t)"))
         pick_words(picked_thirds[2][:], 2, 2 * THIRD, S)
         for i in range(PIECES - 2):
             multiply(1, i)
@@ -177,8 +184,8 @@ def tile_list_tabw_bias_kernel(tc, tab, w, b, offs, out):
         for i in range(PIECES - 2, PIECES):
             multiply(2, i)
         for i in range(PIECES):
-            if i in (3, 5):
-                nc.vector.tensor_scalar(results[i][:], accs[i][:], bias[:], None, op0=ADD)
+            if i in (PIECES - 3, PIECES - 1):
+                nc.vector.tensor_scalar(results[i][:], accs[i][:], bias, None, op0=ADD)
             else:
                 add_bias_on_scalar(i)
-            store(i, nc.scalar if i == 4 else nc.sync)
+            store(i, nc.scalar if i == PIECES - 2 else nc.sync)

@@ -20,15 +20,18 @@ ROW_BASE = 32
 ROW_STEP = 4
 
 THIRD = S // 3
+CUT = 2 * THIRD
 PIECE = THIRD // 2
 EDGES = [0, PIECE // 2] + list(range(PIECE, S + 1, PIECE))
 PIECES = len(EDGES) - 1
-SLIVER = T // 4
+HEAD = T // 4
 
 OVERLAP = 64
-AT_THIRDS = 4 * S
-AT_SCALES = AT_THIRDS - OVERLAP
-AT_WORDS2 = AT_THIRDS + 2 * 4 * THIRD
+W_BYTES = 4 * 4 * M
+AT_W1 = 4 * S
+AT_W2 = AT_W1 + W_BYTES
+AT_WORDS2 = AT_W2 + W_BYTES
+AT_SCALES = AT_W1 - OVERLAP
 SCALES_BYTES = AT_WORDS2 + OVERLAP - AT_SCALES
 
 
@@ -58,18 +61,16 @@ def tile_list_tabw_bias_kernel(tc, tab, w, b, offs, out):
         ]
         w_raw = [
             keep.tile([P, 4, M], F32, name="w_raw0", align_bytes=64),
-            shared.tile([P, 4, M], F32, name="w_raw1", align_bytes=64, offset=AT_THIRDS),
-            shared.tile([P, 4, M], F32, name="w_raw2", align_bytes=64, offset=AT_THIRDS + 4 * THIRD),
+            shared.tile([P, 4, M], F32, name="w_raw1", align_bytes=64, offset=AT_W1),
+            shared.tile([P, 4, M], F32, name="w_raw2", align_bytes=64, offset=AT_W2),
         ]
-        picked_thirds = [
-            keep.tile([P, THIRD], U32, name="third0", align_bytes=64),
-            keep.tile([P, THIRD], U32, name="third1", align_bytes=64),
-            shared.tile([P, THIRD], U32, name="third2", align_bytes=64, offset=AT_THIRDS + 4 * THIRD),
+        picked2 = [
+            keep.tile([P, CUT], U32, name="picked2_first", align_bytes=64),
+            shared.tile([P, S - CUT], U32, name="picked2_last", align_bytes=64, offset=AT_W2),
         ]
         picked_rows = keep.tile([P, S // 4], I32, name="picked_rows", align_bytes=64)
         planes = [keep.tile([P, S // 4], I32, name=f"plane{a}", align_bytes=64) for a in range(PASSES)]
-        w_bf_early = keep.tile([P, M, 4], BF16, name="w_bf_early", align_bytes=64)
-        w_bf_late = keep.tile([P, 2, M, 4], BF16, name="w_bf_late", align_bytes=64)
+        w_bf = [keep.tile([P, M, 4], BF16, name=f"w_bf{a}", align_bytes=64) for a in range(PASSES)]
         w_codes = keep.tile([P, PASSES * M], U32, name="w_codes", align_bytes=64)
         w_scales = keep.tile([P, PASSES * M], U8, name="w_scales", align_bytes=64)
         accs = [psum.tile([M, EDGES[i + 1] - EDGES[i]], F32, name=f"acc{i}") for i in range(PIECES)]
@@ -83,7 +84,6 @@ def tile_list_tabw_bias_kernel(tc, tab, w, b, offs, out):
         def load_words(a, t0, t1):
             table = tab[a, 0 : 512 * T].bitcast(I32).rearrange("(p t) -> p t", p=P)
             nc.sync.dma_start(words[a][:, t0:t1], table[:, t0:t1])
-
 
         def load_w(a):
             rows = w[512 * a : 512 * (a + 1), :].rearrange("(p t) n -> p t n", t=4)
@@ -99,40 +99,36 @@ def tile_list_tabw_bias_kernel(tc, tab, w, b, offs, out):
         def pick_words(dst, a, j0, j1):
             nc.vector.tensor_copy(dst, words[a][:].bitcast(U32).indirect(offsets[:, j0 // 16 : j1 // 16]))
 
-        def round_w(dst, src):
+        def round_w(a):
             nc.scalar.copy(
-                dst.rearrange("p (c i) t -> p c t i", i=4),
-                src.rearrange("p t (c i) -> p c t i", i=4),
+                w_bf[a][:].rearrange("p (c i) t -> p c t i", i=4),
+                w_raw[a][:].rearrange("p t (c i) -> p c t i", i=4),
             )
 
-        def quantise(a0, a1, rounded):
+        def quantise_w(a):
             nc.vector.quantize_mx(
-                out=w_codes[:, M * a0 : M * a1].bitcast(FP8X4),
-                scales=w_scales[:, M * a0 : M * a1],
-                in_=rounded,
+                out=w_codes[:, M * a : M * (a + 1)].bitcast(FP8X4),
+                scales=w_scales[:, M * a : M * (a + 1)],
+                in_=w_bf[a][:].rearrange("p n t -> p (n t)"),
             )
 
         def multiply(a, i):
-            j0, width = EDGES[i], EDGES[i + 1] - EDGES[i]
-            if a == 2:
-                codes = picked_thirds[j0 // THIRD][:, j0 % THIRD : j0 % THIRD + width]
+            j0, j1 = EDGES[i], EDGES[i + 1]
+            if a < 2:
+                codes = picked[a][:, j0:j1]
+            elif j0 < CUT:
+                codes = picked2[0][:, j0:j1]
             else:
-                codes = picked[a][:, j0 : j0 + width]
+                codes = picked2[1][:, j0 - CUT : j1 - CUT]
             nc.tensor.matmul_mx(
                 out=accs[i][:],
                 lhsT=w_codes[:, M * a : M * (a + 1)].bitcast(FP8X4),
                 lhsT_scale=w_scales[:, M * a : M * (a + 1)],
                 rhs=codes.bitcast(FP8X4),
-                rhs_scale=planes[a][:].bitcast(U8)[4 * a : P, j0 : j0 + width],
+                rhs_scale=planes[a][:].bitcast(U8)[4 * a : P, j0:j1],
                 start=(a == 0),
-                stop=(a == 2),
+                stop=(a == PASSES - 1),
             )
-
-        def add_bias_on_scalar(i):
-            nc.scalar.activation(results[i][:], accs[i][:], IDENTITY, bias=bias)
-
-        def store(i, queue):
-            queue.dma_start(out[:, EDGES[i] : EDGES[i + 1]], results[i][:])
 
         nc.vector.memset(scale_window, 0)
         for a in range(PASSES):
@@ -142,10 +138,11 @@ def tile_list_tabw_bias_kernel(tc, tab, w, b, offs, out):
         nc.gpsimd.memset(bias_rows[:], 0.0)
         nc.scalar.dma_start(bias_rows[0:P:32, :], b.rearrange("(q i) -> q i", i=32))
         nc.vector.transpose(bias_cols[:], bias_rows[:])
-        load_words(0, 0, SLIVER)
+
+        load_words(0, 0, HEAD)
         for a in range(PASSES):
             load_scales(a)
-        load_words(0, SLIVER, T)
+        load_words(0, HEAD, T)
         load_w(0)
         load_words(1, 0, T)
 
@@ -163,29 +160,32 @@ def tile_list_tabw_bias_kernel(tc, tab, w, b, offs, out):
                 carry_rows(a, r)
 
         pick_words(picked[0][:], 0, 0, S)
-        round_w(w_bf_early[:], w_raw[0][:])
-        quantise(0, 1, w_bf_early[:].rearrange("p n t -> p (n t)"))
+        round_w(0)
+        quantise_w(0)
         pick_words(picked[1][:], 1, 0, S)
         for i in range(PIECES):
             multiply(0, i)
 
-        pick_words(picked_thirds[0][:], 2, 0, THIRD)
-        pick_words(picked_thirds[1][:], 2, THIRD, 2 * THIRD)
+        pick_words(picked2[0][:], 2, 0, CUT)
         for a in (1, 2):
-            round_w(w_bf_late[:, a - 1], w_raw[a][:])
+            round_w(a)
         for a in (1, 2):
-            quantise(a, a + 1, w_bf_late[:, a - 1].rearrange("p n t -> p (n t)"))
-        pick_words(picked_thirds[2][:], 2, 2 * THIRD, S)
+            quantise_w(a)
+        pick_words(picked2[1][:], 2, CUT, S)
+
+        last_third = range(PIECES - 2, PIECES)
         for i in range(PIECES - 2):
             multiply(1, i)
             multiply(2, i)
-        for i in range(PIECES - 2, PIECES):
-            multiply(1, i)
-        for i in range(PIECES - 2, PIECES):
-            multiply(2, i)
+        for a in (1, 2):
+            for i in last_third:
+                multiply(a, i)
+
+        on_vector = (PIECES - 3, PIECES - 1)
         for i in range(PIECES):
-            if i in (PIECES - 3, PIECES - 1):
+            if i in on_vector:
                 nc.vector.tensor_scalar(results[i][:], accs[i][:], bias, None, op0=ADD)
             else:
-                add_bias_on_scalar(i)
-            store(i, nc.scalar if i == PIECES - 2 else nc.sync)
+                nc.scalar.activation(results[i][:], accs[i][:], IDENTITY, bias=bias)
+            queue = nc.scalar if i == PIECES - 2 else nc.sync
+            queue.dma_start(out[:, EDGES[i] : EDGES[i + 1]], results[i][:])

@@ -20,9 +20,11 @@ ROW_BASE = 32
 ROW_STEP = 4
 
 THIRD = S // 3
-CUT = 2 * THIRD
+CUT = 896
 PIECE = THIRD // 2
-EDGES = [0, PIECE // 2] + list(range(PIECE, S + 1, PIECE))
+EDGES = [0, 128, 256, 512, 768, 896, 1024, 1280, 1536]
+STORES = [0, 128, 256, 512, 768, 1024, 1280, 1536]
+FIRST = EDGES.index(CUT)
 PIECES = len(EDGES) - 1
 HEAD = T // 4
 
@@ -66,7 +68,7 @@ def tile_list_tabw_bias_kernel(tc, tab, w, b, offs, out):
         ]
         picked2 = [
             keep.tile([P, CUT], U32, name="picked2_first", align_bytes=64),
-            shared.tile([P, S - CUT], U32, name="picked2_last", align_bytes=64, offset=AT_W2),
+            shared.tile([P, S - CUT], U32, name="picked2_last", align_bytes=64, offset=AT_WORDS2 - 4 * (S - CUT)),
         ]
         picked_rows = keep.tile([P, S // 4], I32, name="picked_rows", align_bytes=64)
         planes = [keep.tile([P, S // 4], I32, name=f"plane{a}", align_bytes=64) for a in range(PASSES)]
@@ -74,7 +76,7 @@ def tile_list_tabw_bias_kernel(tc, tab, w, b, offs, out):
         w_codes = keep.tile([P, PASSES * M], U32, name="w_codes", align_bytes=64)
         w_scales = keep.tile([P, PASSES * M], U8, name="w_scales", align_bytes=64)
         accs = [psum.tile([M, EDGES[i + 1] - EDGES[i]], F32, name=f"acc{i}") for i in range(PIECES)]
-        results = [keep.tile([M, EDGES[i + 1] - EDGES[i]], F32, name=f"result{i}") for i in range(PIECES)]
+        result = keep.tile([M, S], F32, name="result")
 
         def load_scales(a):
             rows = tab[a, 512 * T : 528 * T].bitcast(I32).rearrange("(q t) -> q t", q=16)
@@ -173,19 +175,22 @@ def tile_list_tabw_bias_kernel(tc, tab, w, b, offs, out):
             quantise_w(a)
         pick_words(picked2[1][:], 2, CUT, S)
 
-        last_third = range(PIECES - 2, PIECES)
-        for i in range(PIECES - 2):
+        last_third = range(FIRST, PIECES)
+        for i in range(FIRST):
             multiply(1, i)
             multiply(2, i)
         for a in (1, 2):
             for i in last_third:
                 multiply(a, i)
 
-        on_vector = (PIECES - 3, PIECES - 1)
+        on_vector = (5, 7,)
         for i in range(PIECES):
+            j0, j1 = EDGES[i], EDGES[i + 1]
             if i in on_vector:
-                nc.vector.tensor_scalar(results[i][:], accs[i][:], bias, None, op0=ADD)
+                nc.vector.tensor_scalar(result[:, j0:j1], accs[i][:], bias, None, op0=ADD)
             else:
-                nc.scalar.activation(results[i][:], accs[i][:], IDENTITY, bias=bias)
-            queue = nc.scalar if i == PIECES - 2 else nc.sync
-            queue.dma_start(out[:, EDGES[i] : EDGES[i + 1]], results[i][:])
+                nc.scalar.activation(result[:, j0:j1], accs[i][:], IDENTITY, bias=bias)
+            if j1 in STORES:
+                j0 = STORES[STORES.index(j1) - 1]
+                queue = nc.scalar if j1 == 1280 else nc.sync
+                queue.dma_start(out[:, j0:j1], result[:, j0:j1])

@@ -19,13 +19,10 @@ PASSES = K // 512
 ROW_BASE = 32
 ROW_STEP = 4
 
-THIRD = S // 3
-CUT = 896
-PIECE = THIRD // 2
-EDGES = [0, 128, 256, 512, 768, 896, 1024, 1280, 1536]
-STORES = [0, 128, 256, 512, 768, 1024, 1280, 1536]
-FIRST = EDGES.index(CUT)
-PIECES = len(EDGES) - 1
+CUT = 768
+LATE_GATHERS = [768, 1024, 1280, 1536]
+BANKS = [0, 128, 384, 768, 1024, 1280, 1408, 1536]
+STORES = [0, 128, 384, 768, 1024, 1280, 1536]
 HEAD = T // 4
 
 OVERLAP = 64
@@ -35,6 +32,19 @@ AT_W2 = AT_W1 + W_BYTES
 AT_WORDS2 = AT_W2 + W_BYTES
 AT_SCALES = AT_W1 - OVERLAP
 SCALES_BYTES = AT_WORDS2 + OVERLAP - AT_SCALES
+
+
+def spans(edges):
+    return list(zip(edges[:-1], edges[1:]))
+
+
+def widths(j0, j1):
+    parts = []
+    for n in (512, 256, 128):
+        while j1 - j0 >= n:
+            parts.append((j0, j0 + n))
+            j0 = j0 + n
+    return parts
 
 
 def tile_list_tabw_bias_kernel(tc, tab, w, b, offs, out):
@@ -75,7 +85,7 @@ def tile_list_tabw_bias_kernel(tc, tab, w, b, offs, out):
         w_bf = [keep.tile([P, M, 4], BF16, name=f"w_bf{a}", align_bytes=64) for a in range(PASSES)]
         w_codes = keep.tile([P, PASSES * M], U32, name="w_codes", align_bytes=64)
         w_scales = keep.tile([P, PASSES * M], U8, name="w_scales", align_bytes=64)
-        accs = [psum.tile([M, EDGES[i + 1] - EDGES[i]], F32, name=f"acc{i}") for i in range(PIECES)]
+        accs = {j0: psum.tile([M, j1 - j0], F32, name=f"acc{j0}") for j0, j1 in spans(BANKS)}
         result = keep.tile([M, S], F32, name="result")
 
         def load_scales(a):
@@ -101,10 +111,10 @@ def tile_list_tabw_bias_kernel(tc, tab, w, b, offs, out):
         def pick_words(dst, a, j0, j1):
             nc.vector.tensor_copy(dst, words[a][:].bitcast(U32).indirect(offsets[:, j0 // 16 : j1 // 16]))
 
-        def round_w(a):
-            nc.scalar.copy(
-                w_bf[a][:].rearrange("p (c i) t -> p c t i", i=4),
-                w_raw[a][:].rearrange("p t (c i) -> p c t i", i=4),
+        def round_w(copy, a, n0, n1):
+            copy(
+                w_bf[a][:, n0:n1, :].rearrange("p (c i) t -> p c t i", i=4),
+                w_raw[a][:, :, n0:n1].rearrange("p t (c i) -> p c t i", i=4),
             )
 
         def quantise_w(a):
@@ -114,34 +124,35 @@ def tile_list_tabw_bias_kernel(tc, tab, w, b, offs, out):
                 in_=w_bf[a][:].rearrange("p n t -> p (n t)"),
             )
 
-        def multiply(a, i):
-            j0, j1 = EDGES[i], EDGES[i + 1]
-            if a < 2:
-                codes = picked[a][:, j0:j1]
-            elif j0 < CUT:
-                codes = picked2[0][:, j0:j1]
-            else:
-                codes = picked2[1][:, j0 - CUT : j1 - CUT]
-            nc.tensor.matmul_mx(
-                out=accs[i][:],
-                lhsT=w_codes[:, M * a : M * (a + 1)].bitcast(FP8X4),
-                lhsT_scale=w_scales[:, M * a : M * (a + 1)],
-                rhs=codes.bitcast(FP8X4),
-                rhs_scale=planes[a][:].bitcast(U8)[4 * a : P, j0:j1],
-                start=(a == 0),
-                stop=(a == PASSES - 1),
-            )
+        def multiply(a, first, last):
+            for j0, j1 in widths(first, last):
+                if a < 2:
+                    codes = picked[a][:, j0:j1]
+                elif j0 < CUT:
+                    codes = picked2[0][:, j0:j1]
+                else:
+                    codes = picked2[1][:, j0 - CUT : j1 - CUT]
+                nc.tensor.matmul_mx(
+                    out=accs[first][:, j0 - first : j1 - first],
+                    lhsT=w_codes[:, M * a : M * (a + 1)].bitcast(FP8X4),
+                    lhsT_scale=w_scales[:, M * a : M * (a + 1)],
+                    rhs=codes.bitcast(FP8X4),
+                    rhs_scale=planes[a][:].bitcast(U8)[4 * a : P, j0:j1],
+                    start=(a == 0 and j0 == first),
+                    stop=(a == PASSES - 1 and j1 == last),
+                )
 
         nc.vector.memset(scale_window, 0)
         for a in range(PASSES):
             nc.vector.memset(planes[a][:], 0)
 
+        load_words(0, 0, HEAD)
         nc.sync.dma_start(offsets[:], offs)
+
         nc.gpsimd.memset(bias_rows[:], 0.0)
         nc.scalar.dma_start(bias_rows[0:P:32, :], b.rearrange("(q i) -> q i", i=32))
         nc.vector.transpose(bias_cols[:], bias_rows[:])
 
-        load_words(0, 0, HEAD)
         for a in range(PASSES):
             load_scales(a)
         load_words(0, HEAD, T)
@@ -150,47 +161,47 @@ def tile_list_tabw_bias_kernel(tc, tab, w, b, offs, out):
 
         nc.vector.tensor_copy(picked_rows[:].bitcast(U8), scale_window.bitcast(U8).indirect(offsets[:]))
 
-        for a in range(PASSES):
-            carry_rows(a, 0)
+        carries = [(a, r) for a in (0, 2, 1) for r in range(4)]
+        for a, r in carries[:2]:
+            carry_rows(a, r)
         load_words(2, 0, T)
-        for r in range(1, 4):
-            carry_rows(0, r)
+        for a, r in carries[2:6]:
+            carry_rows(a, r)
         load_w(1)
         load_w(2)
-        for a in (2, 1):
-            for r in range(1, 4):
-                carry_rows(a, r)
+        for a, r in carries[6:]:
+            carry_rows(a, r)
 
         pick_words(picked[0][:], 0, 0, S)
-        round_w(0)
+        round_w(nc.scalar.copy, 0, 0, M)
         quantise_w(0)
         pick_words(picked[1][:], 1, 0, S)
-        for i in range(PIECES):
-            multiply(0, i)
+        for j0, j1 in spans(BANKS):
+            multiply(0, j0, j1)
 
         pick_words(picked2[0][:], 2, 0, CUT)
-        for a in (1, 2):
-            round_w(a)
+        round_w(nc.scalar.copy, 1, 0, M)
+        round_w(nc.scalar.copy, 2, 0, M // 2)
+        round_w(nc.vector.tensor_copy, 2, M // 2, M)
         for a in (1, 2):
             quantise_w(a)
-        pick_words(picked2[1][:], 2, CUT, S)
+        for j0, j1 in spans(LATE_GATHERS):
+            pick_words(picked2[1][:, j0 - CUT : j1 - CUT], 2, j0, j1)
 
-        last_third = range(FIRST, PIECES)
-        for i in range(FIRST):
-            multiply(1, i)
-            multiply(2, i)
+        waiting = [(j0, j1) for j0, j1 in spans(BANKS) if j0 >= LATE_GATHERS[1]]
+        for j0, j1 in spans(BANKS):
+            if (j0, j1) not in waiting:
+                multiply(1, j0, j1)
+                multiply(2, j0, j1)
         for a in (1, 2):
-            for i in last_third:
-                multiply(a, i)
+            for j0, j1 in waiting:
+                multiply(a, j0, j1)
 
-        on_vector = (5, 7,)
-        for i in range(PIECES):
-            j0, j1 = EDGES[i], EDGES[i + 1]
-            if i in on_vector:
-                nc.vector.tensor_scalar(result[:, j0:j1], accs[i][:], bias, None, op0=ADD)
+        for j0, j1 in spans(BANKS):
+            if j1 == S:
+                nc.vector.tensor_scalar(result[:, j0:j1], accs[j0][:], bias, None, op0=ADD)
             else:
-                nc.scalar.activation(result[:, j0:j1], accs[i][:], IDENTITY, bias=bias)
+                nc.scalar.activation(result[:, j0:j1], accs[j0][:], IDENTITY, bias=bias)
             if j1 in STORES:
-                j0 = STORES[STORES.index(j1) - 1]
-                queue = nc.scalar if j1 == 1280 else nc.sync
-                queue.dma_start(out[:, j0:j1], result[:, j0:j1])
+                first = STORES[STORES.index(j1) - 1]
+                nc.sync.dma_start(out[:, first:j1], result[:, first:j1])

@@ -23,7 +23,7 @@ CUT = 768
 LATE_GATHERS = [768, 1024, 1280, 1536]
 BANKS = [0, 128, 384, 768, 1024, 1280, 1408, 1536]
 STORES = [0, 128, 384, 768, 1024, 1280, 1536]
-HEAD = T // 4
+HEAD = 3 * T // 8
 
 OVERLAP = 64
 W_BYTES = 4 * 4 * M
@@ -161,16 +161,17 @@ def tile_list_tabw_bias_kernel(tc, tab, w, b, offs, out):
 
         nc.vector.tensor_copy(picked_rows[:].bitcast(U8), scale_window.bitcast(U8).indirect(offsets[:]))
 
-        carries = [(a, r) for a in (0, 2, 1) for r in range(4)]
-        for a, r in carries[:2]:
-            carry_rows(a, r)
+        carry_rows(0, 0)
         load_words(2, 0, T)
-        for a, r in carries[2:6]:
-            carry_rows(a, r)
+        carry_rows(0, 1)
+        for a, r in ((2, 2), (1, 3)):
+            carry_rows(a, 0)
+            carry_rows(0, r)
         load_w(1)
         load_w(2)
-        for a, r in carries[6:]:
-            carry_rows(a, r)
+        for r in range(1, 4):
+            for a in (2, 1):
+                carry_rows(a, r)
 
         pick_words(picked[0][:], 0, 0, S)
         round_w(nc.scalar.copy, 0, 0, M)
@@ -198,7 +199,7 @@ def tile_list_tabw_bias_kernel(tc, tab, w, b, offs, out):
                 multiply(a, j0, j1)
 
         for j0, j1 in spans(BANKS):
-            if j1 == S:
+            if j1 in (LATE_GATHERS[-2], S):
                 nc.vector.tensor_scalar(result[:, j0:j1], accs[j0][:], bias, None, op0=ADD)
             else:
                 nc.scalar.activation(result[:, j0:j1], accs[j0][:], IDENTITY, bias=bias)

@@ -19,10 +19,10 @@ PASSES = K // 512
 ROW_BASE = 32
 ROW_STEP = 4
 
-CUT = 768
-LATE_GATHERS = [768, 1024, 1280, 1536]
-BANKS = [0, 128, 384, 768, 1024, 1280, 1408, 1536]
-STORES = [0, 128, 384, 768, 1024, 1280, 1536]
+CUTS = [0, 768, 1024, S]
+LATE_GATHERS = [1024, 1280, 1536]
+BANKS = [0, 128, 384, 640, 768, 1024, 1280, 1408, 1536]
+STORES = [0, 128, 384, 640, 1024, 1280, 1536]
 HEAD = 3 * T // 8
 
 OVERLAP = 64
@@ -77,8 +77,9 @@ def tile_list_tabw_bias_kernel(tc, tab, w, b, offs, out):
             shared.tile([P, 4, M], F32, name="w_raw2", align_bytes=64, offset=AT_W2),
         ]
         picked2 = [
-            keep.tile([P, CUT], U32, name="picked2_first", align_bytes=64),
-            shared.tile([P, S - CUT], U32, name="picked2_last", align_bytes=64, offset=AT_WORDS2 - 4 * (S - CUT)),
+            keep.tile([P, CUTS[1]], U32, name="picked2_first", align_bytes=64),
+            shared.tile([P, CUTS[2] - CUTS[1]], U32, name="picked2_middle", align_bytes=64, offset=AT_W1),
+            shared.tile([P, S - CUTS[2]], U32, name="picked2_last", align_bytes=64, offset=AT_W2),
         ]
         picked_rows = keep.tile([P, S // 4], I32, name="picked_rows", align_bytes=64)
         planes = [keep.tile([P, S // 4], I32, name=f"plane{a}", align_bytes=64) for a in range(PASSES)]
@@ -111,10 +112,10 @@ def tile_list_tabw_bias_kernel(tc, tab, w, b, offs, out):
         def pick_words(dst, a, j0, j1):
             nc.vector.tensor_copy(dst, words[a][:].bitcast(U32).indirect(offsets[:, j0 // 16 : j1 // 16]))
 
-        def round_w(copy, a, n0, n1):
-            copy(
-                w_bf[a][:, n0:n1, :].rearrange("p (c i) t -> p c t i", i=4),
-                w_raw[a][:, :, n0:n1].rearrange("p t (c i) -> p c t i", i=4),
+        def round_w(a):
+            nc.scalar.copy(
+                w_bf[a][:].rearrange("p (c i) t -> p c t i", i=4),
+                w_raw[a][:].rearrange("p t (c i) -> p c t i", i=4),
             )
 
         def quantise_w(a):
@@ -124,14 +125,13 @@ def tile_list_tabw_bias_kernel(tc, tab, w, b, offs, out):
                 in_=w_bf[a][:].rearrange("p n t -> p (n t)"),
             )
 
-        def multiply(a, first, last):
+        def multiply(a, first, last, closing=False):
             for j0, j1 in widths(first, last):
                 if a < 2:
                     codes = picked[a][:, j0:j1]
-                elif j0 < CUT:
-                    codes = picked2[0][:, j0:j1]
                 else:
-                    codes = picked2[1][:, j0 - CUT : j1 - CUT]
+                    part = max(i for i in range(3) if CUTS[i] <= j0)
+                    codes = picked2[part][:, j0 - CUTS[part] : j1 - CUTS[part]]
                 nc.tensor.matmul_mx(
                     out=accs[first][:, j0 - first : j1 - first],
                     lhsT=w_codes[:, M * a : M * (a + 1)].bitcast(FP8X4),
@@ -139,7 +139,7 @@ def tile_list_tabw_bias_kernel(tc, tab, w, b, offs, out):
                     rhs=codes.bitcast(FP8X4),
                     rhs_scale=planes[a][:].bitcast(U8)[4 * a : P, j0:j1],
                     start=(a == 0 and j0 == first),
-                    stop=(a == PASSES - 1 and j1 == last),
+                    stop=(closing and j1 == last),
                 )
 
         nc.vector.memset(scale_window, 0)
@@ -163,40 +163,47 @@ def tile_list_tabw_bias_kernel(tc, tab, w, b, offs, out):
 
         carry_rows(0, 0)
         load_words(2, 0, T)
-        carry_rows(0, 1)
-        for a, r in ((2, 2), (1, 3)):
-            carry_rows(a, 0)
-            carry_rows(0, r)
-        load_w(1)
-        load_w(2)
         for r in range(1, 4):
-            for a in (2, 1):
-                carry_rows(a, r)
+            carry_rows(0, r)
+        carry_rows(1, 0)
+        load_w(1)
+        carry_rows(1, 1)
+        load_w(2)
+        for r in range(2, 4):
+            carry_rows(1, r)
+        for r in range(4):
+            carry_rows(2, r)
 
         pick_words(picked[0][:], 0, 0, S)
-        round_w(nc.scalar.copy, 0, 0, M)
+        round_w(0)
         quantise_w(0)
         pick_words(picked[1][:], 1, 0, S)
         for j0, j1 in spans(BANKS):
             multiply(0, j0, j1)
 
-        pick_words(picked2[0][:], 2, 0, CUT)
-        round_w(nc.scalar.copy, 1, 0, M)
-        round_w(nc.scalar.copy, 2, 0, M // 2)
-        round_w(nc.vector.tensor_copy, 2, M // 2, M)
-        for a in (1, 2):
-            quantise_w(a)
+        pick_words(picked2[0][:], 2, 0, CUTS[1])
+        round_w(1)
+        quantise_w(1)
+        pick_words(picked2[1][:], 2, CUTS[1], CUTS[2])
+        round_w(2)
+        quantise_w(2)
         for j0, j1 in spans(LATE_GATHERS):
-            pick_words(picked2[1][:, j0 - CUT : j1 - CUT], 2, j0, j1)
+            pick_words(picked2[2][:, j0 - CUTS[2] : j1 - CUTS[2]], 2, j0, j1)
 
-        waiting = [(j0, j1) for j0, j1 in spans(BANKS) if j0 >= LATE_GATHERS[1]]
-        for j0, j1 in spans(BANKS):
-            if (j0, j1) not in waiting:
-                multiply(1, j0, j1)
-                multiply(2, j0, j1)
-        for a in (1, 2):
-            for j0, j1 in waiting:
-                multiply(a, j0, j1)
+        tiles = spans(BANKS)
+        early = [t for t in tiles if t[1] <= CUTS[1]]
+        final = [t for t in tiles if t[0] >= LATE_GATHERS[-2]]
+        for j0, j1 in early:
+            multiply(1, j0, j1)
+        for j0, j1 in early:
+            multiply(2, j0, j1, closing=True)
+        for j0, j1 in final:
+            multiply(1, j0, j1)
+        for j0, j1 in tiles[len(early) : -len(final)]:
+            multiply(2, j0, j1)
+            multiply(1, j0, j1, closing=True)
+        for j0, j1 in final:
+            multiply(2, j0, j1, closing=True)
 
         for j0, j1 in spans(BANKS):
             if j1 in (LATE_GATHERS[-2], S):

@@ -161,18 +161,16 @@ def tile_list_tabw_bias_kernel(tc, tab, w, b, offs, out):
 
         nc.vector.tensor_copy(picked_rows[:].bitcast(U8), scale_window.bitcast(U8).indirect(offsets[:]))
 
-        carry_rows(0, 0)
+        carries = [(a, r) for a in range(PASSES) for r in range(4)]
+        for a, r in carries[:2]:
+            carry_rows(a, r)
         load_words(2, 0, T)
-        for r in range(1, 4):
-            carry_rows(0, r)
-        carry_rows(1, 0)
+        for a, r in carries[2:6]:
+            carry_rows(a, r)
         load_w(1)
-        carry_rows(1, 1)
         load_w(2)
-        for r in range(2, 4):
-            carry_rows(1, r)
-        for r in range(4):
-            carry_rows(2, r)
+        for a, r in carries[6:]:
+            carry_rows(a, r)
 
         pick_words(picked[0][:], 0, 0, S)
         round_w(0)
@@ -191,19 +189,15 @@ def tile_list_tabw_bias_kernel(tc, tab, w, b, offs, out):
             pick_words(picked2[2][:, j0 - CUTS[2] : j1 - CUTS[2]], 2, j0, j1)
 
         tiles = spans(BANKS)
-        early = [t for t in tiles if t[1] <= CUTS[1]]
-        final = [t for t in tiles if t[0] >= LATE_GATHERS[-2]]
-        for j0, j1 in early:
+        early, middle, last = tiles[:3], tiles[3:-1], tiles[-1]
+        for j0, j1 in early + [last]:
             multiply(1, j0, j1)
         for j0, j1 in early:
             multiply(2, j0, j1, closing=True)
-        for j0, j1 in final:
-            multiply(1, j0, j1)
-        for j0, j1 in tiles[len(early) : -len(final)]:
+        for j0, j1 in middle:
             multiply(2, j0, j1)
             multiply(1, j0, j1, closing=True)
-        for j0, j1 in final:
-            multiply(2, j0, j1, closing=True)
+        multiply(2, *last, closing=True)
 
         for j0, j1 in spans(BANKS):
             if j1 in (LATE_GATHERS[-2], S):

@@ -161,16 +161,18 @@ def tile_list_tabw_bias_kernel(tc, tab, w, b, offs, out):
 
         nc.vector.tensor_copy(picked_rows[:].bitcast(U8), scale_window.bitcast(U8).indirect(offsets[:]))
 
-        carries = [(a, r) for a in range(PASSES) for r in range(4)]
-        for a, r in carries[:2]:
-            carry_rows(a, r)
+        carry_rows(0, 0)
         load_words(2, 0, T)
-        for a, r in carries[2:6]:
+        for a, r in ((0, 1), (1, 0), (0, 2), (0, 3)):
             carry_rows(a, r)
         load_w(1)
+        carry_rows(1, 1)
         load_w(2)
-        for a, r in carries[6:]:
-            carry_rows(a, r)
+        for r in range(2):
+            carry_rows(1, 2 + r)
+            carry_rows(2, r)
+        for r in range(2, 4):
+            carry_rows(2, r)
 
         pick_words(picked[0][:], 0, 0, S)
         round_w(0)

@@ -163,15 +163,14 @@ def tile_list_tabw_bias_kernel(tc, tab, w, b, offs, out):
 
         carry_rows(0, 0)
         load_words(2, 0, T)
-        for a, r in ((0, 1), (1, 0), (0, 2), (0, 3)):
-            carry_rows(a, r)
+        for r in range(1, 4):
+            carry_rows(0, r)
         load_w(1)
-        carry_rows(1, 1)
+        carry_rows(1, 0)
         load_w(2)
-        for r in range(2):
-            carry_rows(1, 2 + r)
-            carry_rows(2, r)
-        for r in range(2, 4):
+        for r in range(1, 4):
+            carry_rows(1, r)
+        for r in range(4):
             carry_rows(2, r)
 
         pick_words(picked[0][:], 0, 0, S)

@@ -19,17 +19,17 @@ PASSES = K // 512
 ROW_BASE = 32
 ROW_STEP = 4
 
-CUTS = [0, 768, 1024, S]
-LATE_GATHERS = [1024, 1280, 1536]
-BANKS = [0, 128, 384, 640, 768, 1024, 1280, 1408, 1536]
-STORES = [0, 128, 384, 640, 1024, 1280, 1536]
+CUTS = [0, 640, 896, S]
+LATE_GATHERS = [896, 1280, 1536]
+BANKS = [0, 128, 384, 640, 896, 1152, 1280, 1408, 1536]
+STORES = [0, 128, 384, 640, 896, 1280, 1536]
 HEAD = 3 * T // 8
 
 OVERLAP = 64
 W_BYTES = 4 * 4 * M
 AT_W1 = 4 * S
 AT_W2 = AT_W1 + W_BYTES
-AT_WORDS2 = AT_W2 + W_BYTES
+AT_WORDS2 = AT_W2 + 4 * (S - CUTS[2])
 AT_SCALES = AT_W1 - OVERLAP
 SCALES_BYTES = AT_WORDS2 + OVERLAP - AT_SCALES
 

@@ -86,7 +86,11 @@ def tile_list_tabw_bias_kernel(tc, tab, w, b, offs, out):
         w_bf = [keep.tile([P, M, 4], BF16, name=f"w_bf{a}", align_bytes=64) for a in range(PASSES)]
         w_codes = keep.tile([P, PASSES * M], U32, name="w_codes", align_bytes=64)
         w_scales = keep.tile([P, PASSES * M], U8, name="w_scales", align_bytes=64)
-        accs = {j0: psum.tile([M, j1 - j0], F32, name=f"acc{j0}") for j0, j1 in spans(BANKS)}
+        banks = [0, 1, 2, 3, 4, 5, 0, 1]
+        accs = {
+            j0: psum.tile([M, j1 - j0], F32, name=f"acc{j0}", offset=2048 * bank)
+            for bank, (j0, j1) in zip(banks, spans(BANKS))
+        }
         result = keep.tile([M, S], F32, name="result")
 
         def load_scales(a):
@@ -142,6 +146,15 @@ def tile_list_tabw_bias_kernel(tc, tab, w, b, offs, out):
                     stop=(closing and j1 == last),
                 )
 
+        def empty(j0, j1):
+            if j1 in (LATE_GATHERS[-2], S):
+                nc.vector.tensor_scalar(result[:, j0:j1], accs[j0][:], bias, None, op0=ADD)
+            else:
+                nc.scalar.activation(result[:, j0:j1], accs[j0][:], IDENTITY, bias=bias)
+            if j1 in STORES:
+                first = STORES[STORES.index(j1) - 1]
+                nc.sync.dma_start(out[:, first:j1], result[:, first:j1])
+
         nc.vector.memset(scale_window, 0)
         for a in range(PASSES):
             nc.vector.memset(planes[a][:], 0)
@@ -177,7 +190,9 @@ def tile_list_tabw_bias_kernel(tc, tab, w, b, offs, out):
         round_w(0)
         quantise_w(0)
         pick_words(picked[1][:], 1, 0, S)
-        for j0, j1 in spans(BANKS):
+        tiles = spans(BANKS)
+        early, middle, held = tiles[:3], tiles[3:6], tiles[6:]
+        for j0, j1 in early + middle:
             multiply(0, j0, j1)
 
         pick_words(picked2[0][:], 2, 0, CUTS[1])
@@ -189,22 +204,17 @@ def tile_list_tabw_bias_kernel(tc, tab, w, b, offs, out):
         for j0, j1 in spans(LATE_GATHERS):
             pick_words(picked2[2][:, j0 - CUTS[2] : j1 - CUTS[2]], 2, j0, j1)
 
-        tiles = spans(BANKS)
-        early, middle, last = tiles[:3], tiles[3:-1], tiles[-1]
-        for j0, j1 in early + [last]:
+        for j0, j1 in early:
             multiply(1, j0, j1)
         for j0, j1 in early:
             multiply(2, j0, j1, closing=True)
         for j0, j1 in middle:
             multiply(2, j0, j1)
             multiply(1, j0, j1, closing=True)
-        multiply(2, *last, closing=True)
-
-        for j0, j1 in spans(BANKS):
-            if j1 in (LATE_GATHERS[-2], S):
-                nc.vector.tensor_scalar(result[:, j0:j1], accs[j0][:], bias, None, op0=ADD)
-            else:
-                nc.scalar.activation(result[:, j0:j1], accs[j0][:], IDENTITY, bias=bias)
-            if j1 in STORES:
-                first = STORES[STORES.index(j1) - 1]
-                nc.sync.dma_start(out[:, first:j1], result[:, first:j1])
+        for j0, j1 in early + middle:
+            empty(j0, j1)
+        for a in range(PASSES):
+            for j0, j1 in held:
+                multiply(a, j0, j1, closing=(a == 2))
+        for j0, j1 in held:
+            empty(j0, j1)

@@ -208,13 +208,18 @@ def tile_list_tabw_bias_kernel(tc, tab, w, b, offs, out):
             multiply(1, j0, j1)
         for j0, j1 in early:
             multiply(2, j0, j1, closing=True)
-        for j0, j1 in middle:
+        for j0, j1 in early:
+            empty(j0, j1)
+        multiply(2, *middle[0])
+        multiply(1, *middle[0], closing=True)
+        multiply(0, *held[0])
+        multiply(1, *held[0])
+        for j0, j1 in middle[1:]:
             multiply(2, j0, j1)
             multiply(1, j0, j1, closing=True)
-        for j0, j1 in early + middle:
-            empty(j0, j1)
-        for a in range(PASSES):
-            for j0, j1 in held:
-                multiply(a, j0, j1, closing=(a == 2))
+        multiply(0, *held[1])
+        multiply(1, *held[1])
         for j0, j1 in held:
+            multiply(2, j0, j1, closing=True)
+        for j0, j1 in middle + held:
             empty(j0, j1)

@@ -23,7 +23,7 @@ CUTS = [0, 640, 896, S]
 LATE_GATHERS = [896, 1280, 1536]
 BANKS = [0, 128, 384, 640, 896, 1152, 1280, 1408, 1536]
 STORES = [0, 128, 384, 640, 896, 1280, 1536]
-HEAD = 3 * T // 8
+HEAD = 3 * T // 16
 
 OVERLAP = 64
 W_BYTES = 4 * 4 * M
@@ -159,6 +159,7 @@ def tile_list_tabw_bias_kernel(tc, tab, w, b, offs, out):
         for a in range(PASSES):
             nc.vector.memset(planes[a][:], 0)
 
+        load_w(0)
         load_words(0, 0, HEAD)
         nc.sync.dma_start(offsets[:], offs)
 
@@ -169,8 +170,10 @@ def tile_list_tabw_bias_kernel(tc, tab, w, b, offs, out):
         for a in range(PASSES):
             load_scales(a)
         load_words(0, HEAD, T)
-        load_w(0)
         load_words(1, 0, T)
+
+        round_w(0)
+        quantise_w(0)
 
         nc.vector.tensor_copy(picked_rows[:].bitcast(U8), scale_window.bitcast(U8).indirect(offsets[:]))
 
@@ -187,8 +190,6 @@ def tile_list_tabw_bias_kernel(tc, tab, w, b, offs, out):
             carry_rows(2, r)
 
         pick_words(picked[0][:], 0, 0, S)
-        round_w(0)
-        quantise_w(0)
         pick_words(picked[1][:], 1, 0, S)
         tiles = spans(BANKS)
         early, middle, held = tiles[:3], tiles[3:6], tiles[6:]

@@ -25,7 +25,7 @@ BANKS = [0, 128, 384, 640, 896, 1152, 1280, 1408, 1536]
 STORES = [0, 128, 384, 640, 896, 1280, 1536]
 HEAD = 3 * T // 16
 
-OVERLAP = 64
+OVERLAP = 256
 W_BYTES = 4 * 4 * M
 AT_W1 = 4 * S
 AT_W2 = AT_W1 + W_BYTES
@@ -56,42 +56,42 @@ def tile_list_tabw_bias_kernel(tc, tab, w, b, offs, out):
         tc.psum_pool(name="psum", bufs=1) as psum,
     ):
         offsets = lists.tile([P, S // 16], U16, name="offsets")
-        bias_rows = keep.tile([P, 32], F32, name="bias_rows", align_bytes=64)
-        bias_cols = keep.tile([P, 32], F32, name="bias_cols", align_bytes=64)
+        bias_rows = keep.tile([P, 32], F32, name="bias_rows", align_bytes=256)
+        bias_cols = keep.tile([P, 32], F32, name="bias_cols", align_bytes=256)
         bias = bias_cols[:, 0:1]
 
-        scales = shared.tile([P, SCALES_BYTES // 4], I32, name="scales", align_bytes=64, offset=AT_SCALES)
+        scales = shared.tile([P, SCALES_BYTES // 4], I32, name="scales", align_bytes=256, offset=AT_SCALES)
         scale_window = scales[:, 0 : T // 4]
         words = [
-            keep.tile([P, T], I32, name="words0", align_bytes=64),
-            keep.tile([P, T], I32, name="words1", align_bytes=64),
-            shared.tile([P, T], I32, name="words2", align_bytes=64, offset=AT_WORDS2),
+            keep.tile([P, T], I32, name="words0", align_bytes=256),
+            keep.tile([P, T], I32, name="words1", align_bytes=256),
+            shared.tile([P, T], I32, name="words2", align_bytes=256, offset=AT_WORDS2),
         ]
         picked = [
-            shared.tile([P, S], U32, name="picked0", align_bytes=64, offset=0),
-            keep.tile([P, S], U32, name="picked1", align_bytes=64),
+            shared.tile([P, S], U32, name="picked0", align_bytes=256, offset=0),
+            keep.tile([P, S], U32, name="picked1", align_bytes=256),
         ]
         w_raw = [
-            keep.tile([P, 4, M], F32, name="w_raw0", align_bytes=64),
-            shared.tile([P, 4, M], F32, name="w_raw1", align_bytes=64, offset=AT_W1),
-            shared.tile([P, 4, M], F32, name="w_raw2", align_bytes=64, offset=AT_W2),
+            keep.tile([P, 4, M], F32, name="w_raw0", align_bytes=256),
+            shared.tile([P, 4, M], F32, name="w_raw1", align_bytes=256, offset=AT_W1),
+            shared.tile([P, 4, M], F32, name="w_raw2", align_bytes=256, offset=AT_W2),
         ]
         picked2 = [
-            keep.tile([P, CUTS[1]], U32, name="picked2_first", align_bytes=64),
-            shared.tile([P, CUTS[2] - CUTS[1]], U32, name="picked2_middle", align_bytes=64, offset=AT_W1),
-            shared.tile([P, S - CUTS[2]], U32, name="picked2_last", align_bytes=64, offset=AT_W2),
+            keep.tile([P, CUTS[1]], U32, name="picked2_first", align_bytes=256),
+            shared.tile([P, CUTS[2] - CUTS[1]], U32, name="picked2_middle", align_bytes=256, offset=AT_W1),
+            shared.tile([P, S - CUTS[2]], U32, name="picked2_last", align_bytes=256, offset=AT_W2),
         ]
-        picked_rows = keep.tile([P, S // 4], I32, name="picked_rows", align_bytes=64)
-        planes = [keep.tile([P, S // 4], I32, name=f"plane{a}", align_bytes=64) for a in range(PASSES)]
-        w_bf = [keep.tile([P, M, 4], BF16, name=f"w_bf{a}", align_bytes=64) for a in range(PASSES)]
-        w_codes = keep.tile([P, PASSES * M], U32, name="w_codes", align_bytes=64)
-        w_scales = keep.tile([P, PASSES * M], U8, name="w_scales", align_bytes=64)
+        picked_rows = keep.tile([P, S // 4], I32, name="picked_rows", align_bytes=256)
+        planes = [keep.tile([P, S // 4], I32, name=f"plane{a}", align_bytes=256) for a in range(PASSES)]
+        w_bf = [keep.tile([P, M, 4], BF16, name=f"w_bf{a}", align_bytes=256) for a in range(PASSES)]
+        w_codes = keep.tile([P, PASSES * M], U32, name="w_codes", align_bytes=256)
+        w_scales = keep.tile([P, PASSES * M], U8, name="w_scales", align_bytes=256)
         banks = [0, 1, 2, 3, 4, 5, 0, 1]
         accs = {
             j0: psum.tile([M, j1 - j0], F32, name=f"acc{j0}", offset=2048 * bank)
             for bank, (j0, j1) in zip(banks, spans(BANKS))
         }
-        result = keep.tile([M, S], F32, name="result")
+        result = keep.tile([M, S], F32, name="result", align_bytes=256)
 
         def load_scales(a):
             rows = tab[a, 512 * T : 528 * T].bitcast(I32).rearrange("(q t) -> q t", q=16)

import concourse.mybir as mybir

K, M, T, S = 1536, 128, 4096, 1536
FLOPS = 2 * K * M * S

F32 = mybir.dt.float32
BF16 = mybir.dt.bfloat16
I32 = mybir.dt.int32
U32 = mybir.dt.uint32
U16 = mybir.dt.uint16
U8 = mybir.dt.uint8
FP8X4 = mybir.dt.float8_e4m3fn_x4
IDENTITY = mybir.ActivationFunctionType.Identity
ADD = mybir.AluOpType.add

P = 128
PASSES = K // 512

ROW_BASE = 32
ROW_STEP = 4

CUTS = [0, 640, 896, S]
LATE_GATHERS = [896, 1280, 1536]
BANKS = [0, 128, 384, 640, 896, 1152, 1280, 1408, 1536]
STORES = [0, 128, 384, 640, 896, 1280, 1536]
HEAD = 3 * T // 16

OVERLAP = 256
W_BYTES = 4 * 4 * M
AT_W1 = 4 * S
AT_W2 = AT_W1 + W_BYTES
AT_WORDS2 = AT_W2 + 4 * (S - CUTS[2])
AT_SCALES = AT_W1 - OVERLAP
SCALES_BYTES = AT_WORDS2 + OVERLAP - AT_SCALES


def spans(edges):
    return list(zip(edges[:-1], edges[1:]))


def widths(j0, j1):
    parts = []
    for n in (512, 256, 128):
        while j1 - j0 >= n:
            parts.append((j0, j0 + n))
            j0 = j0 + n
    return parts


def tile_list_tabw_bias_kernel(tc, tab, w, b, offs, out):
    nc = tc.nc
    with (
        tc.tile_pool(name="lists", bufs=1) as lists,
        tc.tile_pool(name="keep", bufs=1) as keep,
        tc.tile_pool(name="shared", bufs=1) as shared,
        tc.psum_pool(name="psum", bufs=1) as psum,
    ):
        offsets = lists.tile([P, S // 16], U16, name="offsets")
        bias_rows = keep.tile([P, 32], F32, name="bias_rows", align_bytes=256)
        bias_cols = keep.tile([P, 32], F32, name="bias_cols", align_bytes=256)
        bias = bias_cols[:, 0:1]

        scales = shared.tile([P, SCALES_BYTES // 4], I32, name="scales", align_bytes=256, offset=AT_SCALES)
        scale_window = scales[:, 0 : T // 4]
        words = [
            keep.tile([P, T], I32, name="words0", align_bytes=256),
            keep.tile([P, T], I32, name="words1", align_bytes=256),
            shared.tile([P, T], I32, name="words2", align_bytes=256, offset=AT_WORDS2),
        ]
        picked = [
            shared.tile([P, S], U32, name="picked0", align_bytes=256, offset=0),
            keep.tile([P, S], U32, name="picked1", align_bytes=256),
        ]
        w_raw = [
            keep.tile([P, 4, M], F32, name="w_raw0", align_bytes=256),
            shared.tile([P, 4, M], F32, name="w_raw1", align_bytes=256, offset=AT_W1),
            shared.tile([P, 4, M], F32, name="w_raw2", align_bytes=256, offset=AT_W2),
        ]
        picked2 = [
            keep.tile([P, CUTS[1]], U32, name="picked2_first", align_bytes=256),
            shared.tile([P, CUTS[2] - CUTS[1]], U32, name="picked2_middle", align_bytes=256, offset=AT_W1),
            shared.tile([P, S - CUTS[2]], U32, name="picked2_last", align_bytes=256, offset=AT_W2),
        ]
        picked_rows = keep.tile([P, S // 4], I32, name="picked_rows", align_bytes=256)
        planes = [keep.tile([P, S // 4], I32, name=f"plane{a}", align_bytes=256) for a in range(PASSES)]
        w_bf = [keep.tile([P, M, 4], BF16, name=f"w_bf{a}", align_bytes=256) for a in range(PASSES)]
        w_codes = keep.tile([P, PASSES * M], U32, name="w_codes", align_bytes=256)
        w_scales = keep.tile([P, PASSES * M], U8, name="w_scales", align_bytes=256)
        banks = [0, 1, 2, 3, 4, 5, 0, 1]
        accs = {
            j0: psum.tile([M, j1 - j0], F32, name=f"acc{j0}", offset=2048 * bank)
            for bank, (j0, j1) in zip(banks, spans(BANKS))
        }
        result = keep.tile([M, S], F32, name="result", align_bytes=256)

        def load_scales(a):
            rows = tab[a, 512 * T : 528 * T].bitcast(I32).rearrange("(q t) -> q t", q=16)
            first = ROW_BASE + a
            nc.sync.dma_start(scales[first : first + 16 * ROW_STEP : ROW_STEP, 0 : T // 4], rows)

        def load_words(a, t0, t1):
            table = tab[a, 0 : 512 * T].bitcast(I32).rearrange("(p t) -> p t", p=P)
            nc.sync.dma_start(words[a][:, t0:t1], table[:, t0:t1])

        def load_w(a):
            rows = w[512 * a : 512 * (a + 1), :].rearrange("(p t) n -> p t n", t=4)
            nc.sync.dma_start(w_raw[a][:], rows)

        def carry_rows(a, r):
            first = ROW_BASE + a + ROW_STEP * r
            nc.sync.dma_start(
                planes[a][4 * a + r : P : 32, :],
                picked_rows[first : first + 16 * ROW_STEP : 4 * ROW_STEP, :],
            )

        def pick_words(dst, a, j0, j1):
            nc.vector.tensor_copy(dst, words[a][:].bitcast(U32).indirect(offsets[:, j0 // 16 : j1 // 16]))

        def round_w(a):
            nc.scalar.copy(
                w_bf[a][:].rearrange("p (c i) t -> p c t i", i=4),
                w_raw[a][:].rearrange("p t (c i) -> p c t i", i=4),
            )

        def quantise_w(a):
            nc.vector.quantize_mx(
                out=w_codes[:, M * a : M * (a + 1)].bitcast(FP8X4),
                scales=w_scales[:, M * a : M * (a + 1)],
                in_=w_bf[a][:].rearrange("p n t -> p (n t)"),
            )

        def multiply(a, first, last, closing=False):
            for j0, j1 in widths(first, last):
                if a < 2:
                    codes = picked[a][:, j0:j1]
                else:
                    part = max(i for i in range(3) if CUTS[i] <= j0)
                    codes = picked2[part][:, j0 - CUTS[part] : j1 - CUTS[part]]
                nc.tensor.matmul_mx(
                    out=accs[first][:, j0 - first : j1 - first],
                    lhsT=w_codes[:, M * a : M * (a + 1)].bitcast(FP8X4),
                    lhsT_scale=w_scales[:, M * a : M * (a + 1)],
                    rhs=codes.bitcast(FP8X4),
                    rhs_scale=planes[a][:].bitcast(U8)[4 * a : P, j0:j1],
                    start=(a == 0 and j0 == first),
                    stop=(closing and j1 == last),
                )

        def empty(j0, j1):
            if j1 in (LATE_GATHERS[-2], S):
                nc.vector.tensor_scalar(result[:, j0:j1], accs[j0][:], bias, None, op0=ADD)
            else:
                nc.scalar.activation(result[:, j0:j1], accs[j0][:], IDENTITY, bias=bias)
            if j1 in STORES:
                first = STORES[STORES.index(j1) - 1]
                nc.sync.dma_start(out[:, first:j1], result[:, first:j1])

        nc.vector.memset(scale_window, 0)
        for a in range(PASSES):
            nc.vector.memset(planes[a][:], 0)

        load_w(0)
        load_words(0, 0, HEAD)
        nc.sync.dma_start(offsets[:], offs)

        nc.gpsimd.memset(bias_rows[:], 0.0)
        nc.scalar.dma_start(bias_rows[0:P:32, :], b.rearrange("(q i) -> q i", i=32))
        nc.vector.transpose(bias_cols[:], bias_rows[:])

        for a in range(PASSES):
            load_scales(a)
        load_words(0, HEAD, T)
        load_words(1, 0, T)

        round_w(0)
        quantise_w(0)

        nc.vector.tensor_copy(picked_rows[:].bitcast(U8), scale_window.bitcast(U8).indirect(offsets[:]))

        carry_rows(0, 0)
        load_words(2, 0, T)
        for r in range(1, 4):
            carry_rows(0, r)
        load_w(1)
        carry_rows(1, 0)
        load_w(2)
        for r in range(1, 4):
            carry_rows(1, r)
        for r in range(4):
            carry_rows(2, r)

        pick_words(picked[0][:], 0, 0, S)
        pick_words(picked[1][:], 1, 0, S)
        tiles = spans(BANKS)
        early, middle, held = tiles[:3], tiles[3:6], tiles[6:]
        for j0, j1 in early + middle:
            multiply(0, j0, j1)

        pick_words(picked2[0][:], 2, 0, CUTS[1])
        round_w(1)
        quantise_w(1)
        pick_words(picked2[1][:], 2, CUTS[1], CUTS[2])
        round_w(2)
        quantise_w(2)
        for j0, j1 in spans(LATE_GATHERS):
            pick_words(picked2[2][:, j0 - CUTS[2] : j1 - CUTS[2]], 2, j0, j1)

        for j0, j1 in early:
            multiply(1, j0, j1)
        for j0, j1 in early:
            multiply(2, j0, j1, closing=True)
        for j0, j1 in early:
            empty(j0, j1)
        multiply(2, *middle[0])
        multiply(1, *middle[0], closing=True)
        multiply(0, *held[0])
        multiply(1, *held[0])
        for j0, j1 in middle[1:]:
            multiply(2, j0, j1)
            multiply(1, j0, j1, closing=True)
        multiply(0, *held[1])
        multiply(1, *held[1])
        for j0, j1 in held:
            multiply(2, j0, j1, closing=True)
        for j0, j1 in middle + held:
            empty(j0, j1)
